import numpy as np, ml_dtypes
CORES = [16,17,18,19,32,33,34,35]
N = 8
BF = ml_dtypes.bfloat16
NL, W, B, RO, Q = 116, 3712, 160, 4, 4
def parts(rng):
    X = rng.integers(0, 256, (N, 8, 16, W)); L = rng.integers(0, W, (N, 8, 16, W))
    y = (rng.integers(0, 256, (N, 8, 16, B)) * rng.integers(1, 9, (N, 8, 1, B))) >> 3
    return X, L, y, rng.integers(0, NL, (N, 8, B)), rng.integers(0, 4096, (N, 8, B))
def pack(X, L, y, ln, T):
    return {"xw": np.ascontiguousarray(X.reshape(N, 128, W)).astype(np.float32).astype(BF), "il": np.ascontiguousarray(L.reshape(N, 128, W)).astype(np.int32),
            "y0": np.ascontiguousarray(y.reshape(N, 128, B)).astype(np.float32).astype(BF), "ln0": np.ascontiguousarray(ln).astype(np.int32), "tk0": np.ascontiguousarray(T).astype(np.int32)}
def setup_inputs(rng):
    return pack(*parts(rng))
def setup_inputs_spread(rng):
    X = rng.integers(0, 256, (N, 8, 16, W)) >> rng.integers(0, 9, (N, 8, 1, W)); y = rng.integers(0, 256, (N, 8, 16, B)) >> rng.integers(0, 9, (N, 8, 1, B))
    a = np.exp2(rng.integers(-2, 3, (N, 8, 16, 1))); b = np.exp2(rng.integers(-2, 3, (N, 8, 16, 1)))
    line = np.minimum((NL * rng.random((N, 8, 16, W)) ** a).astype(np.int64), NL - 1); wait = np.minimum((32 * rng.random((N, 8, 16, W)) ** b).astype(np.int64), 31)
    ln = np.minimum((NL * rng.random((N, 8, B)) ** 3).astype(np.int64), NL - 1); T = np.minimum(np.exp2(12 * rng.random((N, 8, B))).astype(np.int64) - 1, 4095)
    return pack(X, 32 * line + wait, y, ln, T)
def ends(rng, top, *shape):
    k = rng.integers(0, 4, shape[:-2] + (1, shape[-1]))
    return top * np.where(k < 2, k, rng.integers(0, 2, shape))
def setup_inputs_ends(rng):
    X = ends(rng, 255, N, 8, 16, W); y = ends(rng, 255, N, 8, 16, B)
    L = np.where(rng.random((N, 8, 16, W)) < 0.8, ends(rng, W - 1, N, 8, 16, W), rng.integers(0, W, (N, 8, 16, W)))
    ln = (NL - 1) * rng.integers(0, 2, (N, 8, B)); T = 4095 * rng.integers(0, 2, (N, 8, B))
    L[..., 0] = 0; L[:, :, 1, 0] = W - 1; L[..., 31] = (W - 1) * rng.integers(0, 2, (N, 8, 16))
    L[..., W - 32] = W - 1; L[:, :, 0, W - 32] = 0; L[..., W - 1] = W - 1; L[:, :, 0, W - 1] = 0
    X[..., 0] = 0; X[..., W - 1] = 0; X[..., W - 2] = 255
    for q in range(N):
        if q == 1:
            for c in (0, 31, W - 2, W - 1): X[q, :, :, c] = 255
            y[q] = np.where(np.argsort(rng.random((8, 16, B)), axis=1) < rng.integers(0, 9, (8, 1, B)), 0, 255)
        else:
            if q == N - 1: y[q] = 0
            for i, l, t, v in ((0, NL - 1, 4095, 0), (B - 1, NL - 1, 4095, 0), (B - 2, NL - 1, 4095, 255), (1, NL - 1, 0, 255), (B - 4, NL - 1, 0, 255), (3, 0, 0, 0), (B - 3, 0, 0, 0)):
                ln[q, :, i] = l; T[q, :, i] = t; y[q, :, :, i] = v
            if q == N - 1: y[q, :7, :, B - 2] = 0
            if q == 2: y[q] = np.where(np.argsort(rng.random((8, 16, B)), axis=1) < rng.integers(9, 17, (8, 1, B)), 0, 255)
    return pack(X, L, y, ln, T)
def setup_inputs_corners(rng):
    X, L, y, ln, T = parts(rng)
    T = np.where(rng.random(T.shape) < 0.7, rng.choice(np.array([0, 15, 16, 31, 32, 4064, 4080, 4095]), T.shape), T)
    ln = np.where(rng.random(ln.shape) < 0.4, rng.choice(np.array([0, NL - 1]), ln.shape), ln)
    for q in range(N):
        for g in range(8):
            e = (q + g) % 8
            if e == 0: ln[q, g] = ln[q, g, 0]; T[q, g] = T[q, g, B - 1]
            elif e == 1: L[q, g] = np.arange(W)
            elif e == 2: L[q, g] = 0
            elif e == 3: L[q, g] = W - 1
            elif e == 4: X[q, g] = np.maximum(X[q, g], 1); y[q, g] = np.where(np.argsort(rng.random((16, B)), axis=0) < rng.integers(8, 10, (1, B)), 0, 255)
            elif e == 5: X[q, g] = 0
            elif e == 6: X[q, g] = 255; y[q, g] = rng.integers(128, 256, (16, B))
            else:
                a = rng.permutation(W)[:B]; ln[q, g] = a >> 5; T[q, g] = (a & 31) + 32 * rng.integers(0, 128, B); h = B // 4
                pl = np.concatenate([np.array([0, W - 1]), 1 + rng.permutation(W - 2)])
                d = rng.permutation(np.concatenate([pl[:h], pl[:h], pl[h:B - h]]))
                L[q, g, 15, a] = (d & 4064) + ((d - T[q, g]) & 31)
    return pack(X, L, y, ln, T)
def setup_inputs_crowd(rng):
    X, L, y, ln, T = parts(rng)
    few = rng.integers(0, NL, (N, 8, 1, 4)); few[:, ::2, :, 0] = NL - 1; few[:, 1::2, :, 1] = 0
    L[:, :, 0:2] = (L[:, :, 0:2] & 31) + 32 * np.take_along_axis(few, rng.integers(0, 4, (N, 8, 1, 2 * W)), 3).reshape(N, 8, 2, W)
    L[:, :, 15:16] = (L[:, :, 15:16] & 31) + 32 * np.take_along_axis(few, rng.integers(0, 2, (N, 8, 1, W)), 3)
    ln = np.take_along_axis(few, rng.integers(0, 4, (N, 8, 1, B)), 3).reshape(N, 8, B)
    p = int(rng.integers(0, N)); q = (p + 1) % N
    X[p] = 0; y[p] = 255 - (rng.integers(0, 128, (8, 16, B)) >> (3 * rng.integers(0, 2, (8, 1, B))))
    X[q] = np.maximum(X[q], 1); y[q] = rng.integers(128, 256, (8, 16, B))
    y[q, int(rng.integers(0, 8)), :, rng.permutation(B)[:int(rng.integers(1, 32))]] = 0
    return pack(X, L, y, ln, T)
def check_inputs(d):
    bad = []
    for k, hi in (("xw", 255), ("il", W - 1), ("y0", 255), ("ln0", NL - 1), ("tk0", 4095)):
        v = np.asarray(d[k]).astype(np.float64)
        if not np.all((v >= 0) & (v <= hi)): bad.append("range of " + k)
        elif not np.all(v == np.floor(v)): bad.append("whole numbers of " + k)
    return bad
def reference(xw, il, y0, ln0, tk0):
    X = xw.astype(np.float32).astype(np.int64).reshape(N, 8, 16, W); L = il.astype(np.int64).reshape(N, 8, 16, W)
    y = y0.astype(np.float32).astype(np.int64).reshape(N, 8, 16, B); ln = ln0.astype(np.int64); T = tk0.astype(np.int64)
    A = np.zeros(N, np.int64)
    for step in range(RO):
        a = 32 * ln + (T & 31)
        c = np.take_along_axis(L, a[:, :, None, :], 3)
        s = (c & 4064) + ((c + T[:, :, None, :]) & 31)
        v = np.take_along_axis(X, np.ascontiguousarray(s.transpose(0, 1, 3, 2)).reshape(N, 8, 1, 16 * B), 3).reshape(N, 8, 16, B, 16 // Q, Q)
        m = np.max(np.min(v, axis=-1), axis=-1)
        z = np.abs(m - y)
        skip = np.add.reduce((z >= y).astype(np.int64), axis=2) >= 9
        ln = np.where(skip, c[:, :, 1], c[:, :, 0]) >> 5
        d = s[:, :, 15]
        T = (T + 1 + (np.add.reduce(z, axis=2) & 31) + (A & 31)[:, None, None]) & 4095
        A = np.add.reduce(skip.reshape(N, 8 * B).astype(np.int64), axis=1)
        y = np.roll(z, 1, axis=0); ln = np.roll(ln, 1, axis=0); T = np.roll(T, 1, axis=0); d = np.roll(d, 1, axis=0)
        for q in range(N):
            for g in range(8):
                p, first = np.unique(d[q, g], return_index=True)
                u = L[q, g]; o = u[:, p]
                u[:, p] = (o & 4064) + ((o + y[q, g][:, first]) & 31)
        if step < RO - 1:
            np.put_along_axis(X, (16 * np.arange(B) + (T & 15))[:, :, None, :], y, 3)
    return {"yw": (L & 31).reshape(N, 128, W).astype(np.float32).astype(BF), "yy": y.reshape(N, 128, B).astype(np.float32).astype(BF), "yl": ln.astype(np.float32), "yt": T.astype(np.float32)}

@@ -1,0 +1,391 @@
+from concourse.mybir import AluOpType, AxisListType, ActivationFunctionType
+
+W, B, RO = 3712, 160, 4
+UN = 464
+SCH = [(0, 56), (56, 112), (112, 144)]
+VCH = (144, 160)
+OFF = 4352.0
+M32 = 402653184.0
+M16 = 201326592.0
+M16K = 1.5 * 2.0 ** 37
+BIG = 2.0 ** 40
+
+SCRATCH = {
+    "ilt": ("sbuf", [128, W], "int32"), "tmp": ("sbuf", [128, W], "int32"),
+    "xt": ("sbuf", [128, W], "bfloat16"), "wy": ("sbuf", [128, W + B], "bfloat16"),
+    "colt": ("sbuf", [128, W], "bfloat16"),
+    "vv": ("sbuf", [128, 16 * B], "bfloat16"), "mn": ("sbuf", [128, 16 * B], "bfloat16"), "mx": ("sbuf", [128, 4 * B], "bfloat16"),
+    "eq": ("sbuf", [128, 10 * B], "bfloat16"), "dru": ("sbuf", [128, B], "uint16"),
+    "y0t": ("sbuf", [128, B], "bfloat16"), "lt": ("sbuf", [128, 64], "int32"), "ltf": ("sbuf", [128, 64], "float32"), "ltt": ("sbuf", [128, 64], "float32"),
+    "wg": ("sbuf", [128, B], "bfloat16"), "wgi": ("sbuf", [128, B], "int32"), "lg": ("sbuf", [128, B], "bfloat16"), "cg": ("sbuf", [128, B], "bfloat16"), "sg": ("sbuf", [128, B], "bfloat16"),
+    "st": ("sbuf", [128, B], "uint16"), "kk": ("sbuf", [128, B], "bfloat16"),
+    "ui": ("sbuf", [128, B], "int32"), "ui2": ("sbuf", [128, B], "int32"), "wold": ("sbuf", [128, B], "bfloat16"),
+    "dws": ("sbuf", [128, B], "float32"), "ps": ("sbuf", [128, B], "float32"), "rs": ("sbuf", [128, B], "float32"), "qs": ("sbuf", [128, B], "float32"),
+    "lose": ("sbuf", [128, 10], "float32"), "lose2": ("sbuf", [128, 10], "float32"), "dd": ("sbuf", [128, 10], "float32"),
+    "d0": ("sbuf", [128, 120], "float32"), "d1": ("sbuf", [128, 120], "float32"), "po": ("sbuf", [128, 120], "float32"),
+    "ta1": ("sbuf", [128, 10], "float32"), "ta2": ("sbuf", [128, 10], "float32"), "ta3": ("sbuf", [128, 10], "float32"), "ta4": ("sbuf", [128, 10], "float32"),
+    "acol": ("sbuf", [128, 1], "float32"), "ai": ("sbuf", [128, 1], "int32"), "ai2": ("sbuf", [128, 1], "int32"), "am": ("sbuf", [128, 1], "float32"),
+    "tfa": ("sbuf", [128, 10], "float32"), "qi": ("sbuf", [128, 10], "int32"), "qi2": ("sbuf", [128, 10], "int32"), "tfn": ("sbuf", [128, 10], "float32"),
+    "aw0": ("sbuf", [128, 10], "uint16"), "tki": ("sbuf", [128, 10], "int32"), "tki2": ("sbuf", [128, 10], "int32"), "l32": ("sbuf", [128, 10], "float32"), "af": ("sbuf", [128, 10], "float32"),
+    "fi": ("sbuf", [128, 20], "int32"), "fi2": ("sbuf", [128, 20], "int32"), "ft": ("sbuf", [128, 32], "float32"), "ftt": ("sbuf", [128, 32], "float32"),
+    "ones": ("sbuf", [128, 128], "bfloat16"), "g1": ("sbuf", [128, 128], "bfloat16"), "gb": ("sbuf", [128, 128], "bfloat16"), "i1": ("sbuf", [128, 128], "bfloat16"),
+    "i32": ("sbuf", [128, 128], "bfloat16"), "in1": ("sbuf", [128, 128], "bfloat16"), "in16": ("sbuf", [128, 128], "bfloat16"),
+    "g8": ("sbuf", [128, 128], "bfloat16"), "gbig": ("sbuf", [128, 128], "bfloat16"), "gw": ("sbuf", [128, 128], "bfloat16"),
+    "e15": ("sbuf", [128, 128], "bfloat16"), "e15x": ("sbuf", [128, 128], "bfloat16"), "e15n": ("sbuf", [128, 128], "bfloat16"),
+    "ea": ("sbuf", [128, 128], "bfloat16"), "eb": ("sbuf", [128, 128], "bfloat16"), "one5": ("sbuf", [128, 128], "float32"),
+    "pq": ("sbuf", [128, B], "int32"), "pq2": ("sbuf", [128, B], "int32"), "mask": ("sbuf", [128, B], "bfloat16"), "q16": ("sbuf", [128, B], "float32"), "rsw": ("sbuf", [128, B], "float32"),
+    "r4": ("sbuf", [128, 896], "bfloat16"), "rs1": ("sbuf", [128, 896], "bfloat16"), "rs2": ("sbuf", [128, 224], "bfloat16"),
+    "pm0": ("sbuf", [128, 10], "int32"), "pm": ("sbuf", [128, 10], "int32"), "pmf": ("sbuf", [128, 10], "float32"), "c16": ("sbuf", [128, 10], "int32"),
+    "li": ("sbuf", [128, 10], "float32"), "li16": ("sbuf", [128, 10], "float32"), "dum": ("sbuf", [128, 10], "float32"),
+    "cc": ("sbuf", [128, 24], "float32"), "bt": ("sbuf", [128, 8], "int32"),
+}
+for _t in range(RO):
+    SCRATCH["m1_%d" % _t] = ("sbuf", [128, 20], "uint16")
+    SCRATCH["zs_%d" % _t] = ("sbuf", [128, B], "bfloat16")
+    SCRATCH["m3_%d" % _t] = ("sbuf", [128, 20], "uint16")
+    SCRATCH["r1_%d" % _t] = ("sbuf", [128, 20], "uint16")
+    SCRATCH["rz_%d" % _t] = ("sbuf", [128, B], "bfloat16")
+    SCRATCH["r3_%d" % _t] = ("sbuf", [128, 20], "uint16")
+for _t in range(8):
+    SCRATCH["b%d" % _t] = ("psum", [128, 512], "float32")
+SEMAPHORES = ["qV", "qS", "qT", "qP", "loc", "dil0", "dil1", "dil2", "dil3", "dx", "dy", "dlt", "oyy", "oyw", "osm", "osn"]
+SEMAPHORES += ["a%s_%d" % (m, t) for m in ("1", "z", "3") for t in range(RO)]
+
+
+def rank_program(g, core, T, topo):
+    rank = T.rank_of(core)
+    if rank is None:
+        return
+    n = len(T.cores)
+    nxt, prv = T.cores[(rank + 1) % n], T.cores[(rank - 1) % n]
+    OP, AF = AluOpType, ActivationFunctionType
+    ADD, SUB, MUL, MAX, MIN, EQ, GE, GT = OP.add, OP.subtract, OP.mult, OP.max, OP.min, OP.is_equal, OP.is_ge, OP.is_gt
+    AND, SHR = OP.bitwise_and, OP.arith_shift_right
+    eng = {"V": g.vector, "S": g.scalar, "T": g.tensor, "P": g, "Y": g.sync}
+    know = {e: {} for e in eng}
+    tot, lastw, readers = {}, {}, {}
+
+    def waits(e, r, w):
+        deps = []
+        for k in r:
+            deps += lastw.get(k, [])
+        for k in w:
+            deps += lastw.get(k, []) + readers.get(k, [])
+        deps = [d for d in deps if know[e].get(d[0], 0) < d[1] and not (e == "T" and d[0] == "qT")]
+        need = {}
+        for d in deps:
+            if d[0] not in need or need[d[0]][1] < d[1]:
+                need[d[0]] = d
+        keep = [d for d in need.values() if not any(o is not d and o[2].get(d[0], 0) >= d[1] for o in need.values())]
+        for d in keep:
+            eng[e].wait_ge(T.sem[d[0]], d[1])
+        for d in need.values():
+            for s, v in list(d[2].items()) + [(d[0], d[1])]:
+                know[e][s] = max(know[e].get(s, 0), v)
+
+    def done(e, inst, r, w, sem, inc):
+        tot[sem] = tot.get(sem, 0) + inc
+        inst.then_inc(T.sem[sem], inc)
+        snap = dict(know[e])
+        snap[sem] = tot[sem]
+        ev = (sem, tot[sem], snap)
+        for k in r:
+            readers.setdefault(k, []).append(ev)
+        for k in w:
+            lastw[k] = [ev]
+            readers[k] = []
+
+    def do(e, fn, r, w):
+        waits(e, r, w)
+        done(e, fn(eng[e]), r, w, "q" + e, 1)
+
+    def dma(e, out, in_, r, w, sem):
+        waits(e, r, w)
+        done(e, eng[e].dma_start(out, in_), r, w, sem, 16)
+
+    def tt(out, a, b, op, r, w):
+        do("V", lambda v: v.tensor_tensor(out, a, b, op), r, w)
+
+    def ts(out, a, s1, o1, r, w, s2=None, o2=None):
+        if o2 is None:
+            do("V", lambda v: v.tensor_scalar(out, a, s1, None, o1), r, w)
+        else:
+            do("V", lambda v: v.tensor_scalar(out, a, s1, s2, o1, o2), r, w)
+
+    def cp(out, a, r, w):
+        do("V", lambda v: v.tensor_copy(out, a), r, w)
+
+    def ms(ap, val, w):
+        do("V", lambda v: v.memset(ap, val), [], w)
+
+    def scan(out, x0, x1, o0, o1, r, w):
+        do("V", lambda v: v.tensor_tensor_scan(out, x0, x1, 0.0, o0, o1), r, w)
+
+    def mm(out, lhs, rhs, start, stop, r, w):
+        do("T", lambda v: v.matmul(out, lhs, rhs, start, stop), r, w)
+
+    def act(out, in_, func, r, w, bias=None):
+        if bias is None:
+            do("S", lambda v: v.activation(out, in_, func), r, w)
+        else:
+            do("S", lambda v: v.activation(out, in_, func, bias=bias), r, w)
+
+    sent = [0]
+    rid, pid, _se = topo.addr(nxt)
+    msk, ne = topo.mask(core, nxt), len(topo.engines(core, nxt))
+    na = len(topo.engines(prv, core))
+
+    def send(out, in_, r, sem):
+        waits("P", r, [])
+        g.remote_dma(out, in_, T.sem[sem], T.sem.loc, pid, rid, msk)
+        sent[0] += ne
+
+    def arrives(tok, sem):
+        lastw[tok] = [(sem, na, {sem: na})]
+        tot[sem] = na
+
+    ms(T.lt[:], 0, ["lt"])
+    for q in range(4):
+        c = q * 928
+        dma("Y", T.ilt[:, c:c + 928], T.il[:, c:c + 928], [], ["il%d" % q], "dil%d" % q)
+    dma("Y", T.xt[:], T.xw[:], [], ["x"], "dx")
+    lts = []
+    for a in range(4):
+        for h in range(2):
+            for j, src in ((0, T.ln0), (1, T.tk0)):
+                tk = "lt%d%d%d" % (a, h, j)
+                lastw[tk] = lastw["lt"]
+                dma("S", T.lt[32 * a:32 * a + 10, 32 * j + 16 * h:32 * j + 16 * h + 16], src[2 * a + h:2 * a + h + 1, :], [], [tk], "dlt")
+                lts.append(tk)
+    dma("S", T.y0t[:], T.y0[:], [], ["y0"], "dy")
+
+    def pool(fn, r, w):
+        do("P", fn, r, w)
+    ms(T.ones[:], 1.0, ["ones"])
+    pool(lambda p: p.iota(T.pq[:], [[0, 10], [1, 16]], 128, -1), [], ["pq"])
+    pool(lambda p: p.iota(T.pm0[:], [[0, 10]], 0, 1), [], ["pm0"])
+    pool(lambda p: p.iota(T.c16[:], [[16, 10]], 0, 0), [], ["c16"])
+    pool(lambda p: p.iota(T.q16[:], [[0, 10], [1, 16]], 0, 0, allow_small_or_imprecise_dtypes=True), [], ["q16"])
+    pool(lambda p: p.affine_select(T.i1[:], T.ones[:], [[-1, 128]], EQ, 0.0, 0, 1), ["ones"], ["i1"])
+    pool(lambda p: p.affine_select(T.gb[:], T.ones[:], [[-16, 8], [0, 16]], GE, 0.0, 0, 1), ["ones"], ["gb"])
+    pool(lambda p: p.affine_select(T.g1[:], T.gb[:], [[16, 8], [0, 16]], GE, 0.0, 15, -1), ["gb"], ["g1"])
+    pool(lambda p: p.iota(T.r4[:], [[0, 224], [1, 4]], 0, 0, allow_small_or_imprecise_dtypes=True), [], ["r4"])
+    pool(lambda p: p.iota(T.colt[:], [[0, 116], [1, 32]], -16, 0, allow_small_or_imprecise_dtypes=True), [], ["colt"])
+
+    ms(T.wy[:, W:W + B], 0.0, ["wyd"])
+    ms(T.ft[:], 0.0, ["ft"])
+    ms(T.one5[:], 512.0, ["one5"])
+    ms(T.acol[:], 0.0, ["acol"])
+    ms(T.am[:], 0.0, ["am"])
+    ms(T.d0[:], 1.0, ["d0c"])
+    ms(T.d1[:], 0.0, ["d1c"])
+    d0c = lambda lo, hi, v: ms(T.d0[:, lo:hi:6], v, ["d0c"])
+    d0c(0, 60, 0.0); d0c(5, 60, -1.0)
+    d0c(60, 120, 0.0); d0c(61, 120, 0.0); d0c(62, 120, 0.0); d0c(65, 120, -1.0)
+    d1c = lambda lo, hi, v: ms(T.d1[:, lo:hi:6], v, ["d1c"])
+    d1c(3, 60, M32); d1c(4, 60, -M32); d1c(63, 120, M16); d1c(64, 120, -M16)
+    for k in ("d1b", "d1s", "d1x1", "d1x2", "d1x3", "d1x4"):
+        lastw[k] = lastw["d1c"]
+    lastw["d0s"] = lastw["d0c"]
+    ts(T.pq2[:], T.pq[:], 15, AND, ["pq"], ["pq2"])
+    ts(T.mask[:], T.pq2[:], 0.0, GT, ["pq2"], ["mask"], -(2.0 ** 60), MUL)
+    ts(T.rsw[:], T.q16[:], -0.5, ADD, ["q16"], ["rsw"], 1e27, MUL)
+    ts(T.pm[:], T.pm0[:], 15, AND, ["pm0"], ["pm"])
+    cp(T.pmf[:], T.pm[:], ["pm"], ["pmf"])
+    tt(T.li[:], T.pm[:], T.c16[:], ADD, ["pm", "c16"], ["li"])
+    ts(T.li16[:], T.li[:], 16.0, MUL, ["li"], ["li16"], OFF, ADD)
+    ts(T.dum[:], T.li[:], W + OFF, ADD, ["li"], ["dum"])
+    ts(T.i32[:], T.i1[:], 32.0, MUL, ["i1"], ["i32"])
+    ts(T.in1[:], T.i1[:], -1.0, MUL, ["i1"], ["in1"])
+    ts(T.in16[:], T.i1[:], -16.0, MUL, ["i1"], ["in16"])
+    ts(T.g8[:], T.g1[:], 8192.0, MUL, ["g1"], ["g8"])
+    ts(T.gbig[:], T.g1[:], BIG, MUL, ["g1"], ["gbig"])
+    cc = lambda j: T.cc[:, j:j + 1]
+    pf = T.pmf[:, 0:1]
+    ts(cc(0), pf, 15.0, EQ, ["pmf"], ["cc0"])
+    ts(cc(1), pf, 0.0, EQ, ["pmf"], ["cc1"])
+    ts(cc(2), pf, 1.0, EQ, ["pmf"], ["cc2"])
+    tt(cc(3), cc(1), cc(2), SUB, ["cc1", "cc2"], ["cc3"])
+    ts(T.e15[:], T.g1[:], cc(0), MUL, ["g1", "cc0"], ["e15"])
+    ts(T.e15x[:], T.g1[:], cc(0), MUL, ["g1", "cc0"], ["e15x"], 32.0, MUL)
+    ts(T.e15n[:], T.g1[:], cc(0), MUL, ["g1", "cc0"], ["e15n"], -16.0, MUL)
+    ts(T.ea[:], T.g1[:], cc(3), MUL, ["g1", "cc3"], ["ea"], 16384.0, MUL)
+    ts(T.eb[:], T.g1[:], cc(1), MUL, ["g1", "cc1"], ["eb"], 32.0, MUL)
+    for k in range(4):
+        f = float(4 ** (2 ** k))
+        ts(T.bt[:, k:k + 1], T.pm[:, 0:1], k, SHR, ["pm"], ["bt%d" % k], 1, AND)
+        ts(cc(4 + k), T.bt[:, k:k + 1], 1.0 - f, MUL, ["bt%d" % k], ["cc%d" % (4 + k)], f, ADD)
+    tt(cc(8), cc(4), cc(5), MUL, ["cc4", "cc5"], ["cc8"])
+    tt(cc(9), cc(6), cc(7), MUL, ["cc6", "cc7"], ["cc9"])
+    tt(cc(10), cc(8), cc(9), MUL, ["cc8", "cc9"], ["cc10"])
+    ts(cc(11), cc(10), 2.0, MUL, ["cc10"], ["cc11"])
+    ts(T.gw[:], T.g1[:], cc(10), MUL, ["g1", "cc10"], ["gw"])
+    ts(T.rs1[:], T.r4[:], 0.0, EQ, ["r4"], ["rs1"], 512.0, MUL)
+    ts(T.rs2[:], T.r4[:, 0:224], 0.0, GT, ["r4"], ["rs2"], 512.0, MUL)
+    cp(T.ltf[:], T.lt[:], ["lt"] + lts, ["ltf"])
+    do("V", lambda v: v.transpose(T.ltt[:], T.ltf[:]), ["ltf"], ["ltt"])
+    cp(T.tki[:], T.ltt[:, 32:42], ["ltt"], ["tki"])
+    ts(T.l32[:], T.ltt[:, 0:10], 32.0, MUL, ["ltt"], ["l32"])
+    ts(T.tki2[:], T.tki[:], 31, AND, ["tki"], ["tki2"])
+    tt(T.af[:], T.l32[:], T.tki2[:], ADD, ["l32", "tki2"], ["af"])
+    cp(T.aw0[:], T.af[:], ["af"], ["aw_0"])
+
+    WY = ["wy%d" % u for u in range(8)] + ["wyd"]
+    IL = ["il0", "il1", "il2", "il3"]
+
+    def unit(u):
+        c = u * UN
+        ts(T.tmp[:, c:c + UN], T.ilt[:, c:c + UN], 31, AND, ["il%d" % (u // 2)], ["tmp%d" % u])
+        cp(T.wy[:, c:c + UN], T.tmp[:, c:c + UN], ["tmp%d" % u], ["wy%d" % u])
+
+    for u in range(5):
+        unit(u)
+
+    def rewrite_prep(t):
+        d = T["r1_%d" % (t - 1)][:, 0:10]
+        cp(T.wold[:], T.wy[:].indirect(d), WY + ["r1_%d" % (t - 1)], ["wold"])
+        mm(T.b2[:, 0:B], T.i1[:], T.wold[:], True, True, ["i1", "wold"], ["b2"])
+
+    def rewrite(t):
+        tz = "rz_%d" % (t - 1)
+        d = T["r1_%d" % (t - 1)][:, 0:10]
+        tt(T.ui[:], T.b2[:, 0:B], T[tz][:], ADD, ["b2", tz], ["ui"])
+        ts(T.ui2[:], T.ui[:], 31, AND, ["ui"], ["ui2"])
+        cp(T.wy[:].indirect(d), T.ui2[:], ["ui2", "r1_%d" % (t - 1)], WY)
+
+    b = [T["b%d" % j] for j in range(8)]
+    P = lambda j: b[j][:, 0:B]
+    for t in range(RO):
+        last = t == RO - 1
+        m1, zs, m3 = T["m1_%d" % t], T["zs_%d" % t], T["m3_%d" % t]
+        if t == 0:
+            y, ty, aw, taw = T.y0t[:], "y0", T.aw0[:], "aw_0"
+            tfin, ttf = T.ltt[:, 32:42], "ltt"
+        else:
+            y, ty = T["rz_%d" % (t - 1)][:], "rz_%d" % (t - 1)
+            aw, taw = T["r3_%d" % (t - 1)][:, 0:10], "r3_%d" % (t - 1)
+            tfin, ttf = T["r1_%d" % t][:, 10:20], "r1_%d" % t
+        for k, s in (("r1", "a1"), ("rz", "az"), ("r3", "a3")):
+            arrives("%s_%d" % (k, t), "%s_%d" % (s, t))
+        mm(b[6][:, 0:B], T.i1[:], y, True, True, ["i1", ty], ["b6"])
+        for j in (3, 4, 5, 7):
+            mm(P(j), T.i1[:], T.mask[:], True, False, ["i1", "mask"], ["b%d" % j])
+        if t > 0:
+            rewrite(t)
+        if t == 0:
+            ts(T.wgi[:], T.ilt[:].indirect(aw), 31, AND, IL + [taw], ["wgi"])
+            cp(T.wg[:], T.wgi[:], ["wgi"], ["wg"])
+        else:
+            cp(T.wg[:], T.wy[:].indirect(aw), WY + [taw], ["wg"])
+        act(T.cg[:], T.colt[:].indirect(aw), AF.Copy, ["colt", taw], ["cg"])
+        ts(T.lg[:], T.ilt[:].indirect(aw), 0.03125, MUL, IL + [taw], ["lg"], 136.0 - 31.0 / 64.0, ADD)
+        if t > 0:
+            cp(T.xt[:, 0:16 * B].indirect(T["r3_%d" % (t - 1)][:, 10:20]), y, [ty, taw], ["x"])
+        mm(P(0), T.i1[:], T.wg[:], True, False, ["i1", "wg"], ["b0"])
+        mm(P(0), T.i1[:], T.cg[:], False, True, ["i1", "cg"], ["b0"])
+        act(T.sg[:], P(0), AF.Sign, ["b0"], ["sg"], bias=-15.5)
+        mm(P(1), T.i1[:], T.wg[:], True, False, ["i1", "wg"], ["b1"])
+        mm(P(1), T.i1[:], T.cg[:], False, False, ["i1", "cg"], ["b1"])
+        mm(P(1), T.i32[:], T.lg[:], False, False, ["i32", "lg"], ["b1"])
+        mm(P(1), T.in16[:], T.sg[:], False, True, ["in16", "sg"], ["b1"])
+        for j, first in ((2, True), (3, False)):
+            mm(P(j), T.e15[:], T.wg[:], first, False, ["e15", "wg"], ["b%d" % j])
+            mm(P(j), T.e15[:], T.cg[:], False, False, ["e15", "cg"], ["b%d" % j])
+            mm(P(j), T.e15x[:], T.lg[:], False, False, ["e15x", "lg"], ["b%d" % j])
+            mm(P(j), T.e15n[:], T.sg[:], False, True, ["e15n", "sg"], ["b%d" % j])
+        mm(P(4), T.ea[:], T.lg[:], False, False, ["ea", "lg"], ["b4"])
+        mm(P(4), T.eb[:], T.lg[:], False, True, ["eb", "lg"], ["b4"])
+        ts(T.st[:], P(1), -OFF, ADD, ["b1"], ["st"])
+        for j, (lo, hi) in enumerate(SCH):
+            act(T.vv[:, 16 * lo:16 * hi], T.xt[:].indirect(T.st[:, lo:hi]), AF.Copy, ["x", "st"], ["vv%d" % j])
+        if t == 0:
+            unit(5)
+            unit(6)
+        cp(T.dru[:], P(2), ["b2"], ["dru"])
+        scan(T.dws[:], T.rsw[:], P(3), MIN, MAX, ["rsw", "b3"], ["dws"])
+        for c in range(10):
+            nn = B - 16 * c
+            e0 = c * B
+            ts(T.eq[:, e0:e0 + nn], T.dru[:, 16 * c:B], T.dws[:, 16 * c + 15:16 * c + 16], EQ, ["dru", "dws"], ["eq%d" % c])
+            mm(b[5][:, 16 * c:16 * c + 16], T.gw[:], T.eq[:, e0:e0 + 16], False, c == 9, ["gw", "eq%d" % c], ["b5"])
+            if c < 9:
+                mm(b[5][:, 16 * c + 16:B], T.gbig[:], T.eq[:, e0 + 16:e0 + nn], False, False, ["gbig", "eq%d" % c], ["b5"])
+        lo, hi = VCH
+        cp(T.vv[:, 16 * lo:16 * hi], T.xt[:].indirect(T.st[:, lo:hi]), ["x", "st"], ["vv3"])
+        scan(T.ps[:], T.rsw[:], P(4), MIN, MAX, ["rsw", "b4"], ["ps"])
+        ts(T.d0[:, 1:60:6], T.ps[:, 15:B:16], M16K, ADD, ["ps"], ["d0s"], M16K, SUB)
+        scan(T.rs[:], T.rsw[:], P(5), MIN, MAX, ["rsw", "b5"], ["rs"])
+        tt(T.d1[:, 1:60:6], T.d0[:, 1:60:6], T.ps[:, 15:B:16], SUB, ["d0s", "ps"], ["d1s"])
+        ts(T.lose[:], T.rs[:, 15:B:16], cc(11), GE, ["rs", "cc11"], ["lose"])
+        ts(T.ta1[:], aw, T.acol[:], ADD, [taw, "acol"], ["ta1"], 1.0 - 15.5, ADD)
+        ts(T.ta2[:], aw, T.acol[:], ADD, [taw, "acol"], ["ta2"], 1.0, ADD)
+        tt(T.lose2[:], T.lose[:], T.dum[:], MUL, ["lose", "dum"], ["lose2"])
+        if not last:
+            ts(T.ta3[:], aw, T.acol[:], ADD, [taw, "acol"], ["ta3"], 1.0 - 7.5, ADD)
+            tt(T.ta4[:], T.ta2[:], T.li16[:], ADD, ["ta2", "li16"], ["ta4"])
+        tt(T.dd[:], T.lose2[:], T.dws[:, 15:B:16], MAX, ["lose2", "dws"], ["dd"])
+        ts(m1[:, 0:10], T.dd[:], -OFF, ADD, ["dd"], ["m1d_%d" % t])
+        wid = 10 if t == 0 else 20
+        send(T["r1_%d" % t][:, 0:wid], m1[:, 0:wid], ["m1d_%d" % t] + (["m1t_%d" % t] if t else []), "a1_%d" % t)
+        for j, (lo, hi) in list(enumerate(SCH))[:-1] + [(3, VCH)] + [(2, SCH[2])]:
+            l = hi - lo
+            scan(T.mn[:, 16 * lo:16 * hi], T.rs1[:, 0:16 * l], T.vv[:, 16 * lo:16 * hi], MAX, MIN, ["rs1", "vv%d" % j], ["mn%d" % j])
+            scan(T.mx[:, 4 * lo:4 * hi], T.rs2[:, 0:4 * l], T.mn[:, 16 * lo + 3:16 * hi:4], MIN, MAX, ["rs2", "mn%d" % j], ["mx%d" % j])
+        mm(b[6][:, 256:256 + B], T.in1[:], y, True, False, ["in1", ty], ["b6"])
+        mm(b[6][:, 256:256 + B], T.i1[:], T.mx[:, 3:4 * B:4], False, True, ["i1", "mx0", "mx1", "mx2", "mx3"], ["b6"])
+        act(zs[:], b[6][:, 256:256 + B], AF.Abs, ["b6"], ["zs_%d" % t])
+        send(T["rz_%d" % t][:], zs[:], ["zs_%d" % t], "az_%d" % t)
+        tt(T.kk[:], zs[:], b[6][:, 0:B], GE, ["zs_%d" % t, "b6"], ["kk"])
+        mm(P(7), T.g1[:], zs[:], False, False, ["g1", "zs_%d" % t], ["b7"])
+        mm(P(7), T.g8[:], T.kk[:], False, True, ["g8", "kk"], ["b7"])
+        scan(T.qs[:], T.rsw[:], P(7), MIN, MAX, ["rsw", "b7"], ["qs"])
+        q = T.qs[:, 15:B:16]
+        ts(T.d1[:, 0:60:6], q, 73727.5, GE, ["qs"], ["d1b"], 1.0 / 512.0, MUL)
+        tt(T.d1[:, 2:60:6], q, T.ta1[:], ADD, ["qs", "ta1"], ["d1x1"])
+        tt(T.d1[:, 5:60:6], q, T.ta2[:], ADD, ["qs", "ta2"], ["d1x2"])
+
+        def clock(out):
+            cp(T.qi[:], q, ["qs"], ["qi"])
+            ts(T.tfa[:], tfin, T.am[:], ADD, [ttf, "am"], ["tfa"], 1.0, ADD)
+            ts(T.qi2[:], T.qi[:], 31, AND, ["qi"], ["qi2"])
+            tt(T.tfn[:], T.tfa[:], T.qi2[:], ADD, ["tfa", "qi2"], ["tfn"])
+            cp(out[0], T.tfn[:], ["tfn"], [out[1]])
+        toks = ["d0c", "d0s", "d1c", "d1s", "d1b", "d1x1", "d1x2"]
+        if last:
+            scan(T.po[:, 0:60], T.d0[:, 0:60], T.d1[:, 0:60], MUL, ADD, toks, ["po"])
+            ts(m3[:, 0:10], T.po[:, 5:60:6], -OFF, ADD, ["po"], ["m3a"])
+            clock((m3[:, 10:20], "m3b"))
+            send(T["r3_%d" % t][:], m3[:], ["m3a", "m3b"], "a3_%d" % t)
+        else:
+            tt(T.d1[:, 62:120:6], q, T.ta3[:], ADD, ["qs", "ta3"], ["d1x3"])
+            tt(T.d1[:, 65:120:6], q, T.ta4[:], ADD, ["qs", "ta4"], ["d1x4"])
+            scan(T.po[:], T.d0[:], T.d1[:], MUL, ADD, toks + ["d1x3", "d1x4"], ["po"])
+            ts(m3[:], T.po[:, 5:120:6], -OFF, ADD, ["po"], ["m3_%d" % t])
+            send(T["r3_%d" % t][:], m3[:], ["m3_%d" % t], "a3_%d" % t)
+            mm(b[0][:, 0:10], T.one5[:], T.d1[:, 0:60:6], True, True, ["one5", "d1b"], ["b0"])
+            clock((T["m1_%d" % (t + 1)][:, 10:20], "m1t_%d" % (t + 1)))
+            do("V", lambda v: v.tensor_reduce(T.acol[:], b[0][:, 0:10], AxisListType.X, ADD), ["b0"], ["acol"])
+            if t == 0:
+                unit(7)
+        rewrite_prep(t + 1)
+        if not last:
+            cp(T.ai[:], T.acol[:], ["acol"], ["ai"])
+            ts(T.ai2[:], T.ai[:], 31, AND, ["ai"], ["ai2"])
+            cp(T.am[:], T.ai2[:], ["ai2"], ["am"])
+    rewrite(RO)
+    dma("Y", T.yw[:], T.wy[:, 0:W], WY, [], "oyw")
+    dma("S", T.yy[:], T["rz_3"][:], ["rz_3"], [], "oyy")
+    cp(T.fi[:], T["r3_3"][:], ["r3_3"], ["fi"])
+    ts(T.fi2[:, 0:10], T.fi[:, 0:10], 5, SHR, ["fi"], ["fi2a"])
+    ts(T.fi2[:, 10:20], T.fi[:, 10:20], 4095, AND, ["fi"], ["fi2b"])
+    cp(T.ft[:, 0:20], T.fi2[:], ["fi2a", "fi2b"], ["ft"])
+    do("V", lambda v: v.transpose(T.ftt[:], T.ft[:]), ["ft"], ["ftt"])
+    for a in range(4):
+        for h in range(2):
+            r = 2 * a + h
+            dma("S", T.yl[r:r + 1, :], T.ftt[32 * a:32 * a + 10, 16 * h:16 * h + 16], ["ftt"], [], "osm")
+            dma("Y", T.yt[r:r + 1, :], T.ftt[32 * a + 10:32 * a + 20, 16 * h:16 * h + 16], ["ftt"], [], "osn")
+    g.wait_ge(T.sem.loc, sent[0])
+    for s, v in tot.items():
+        if know["P"].get(s, 0) < v:
+            g.wait_ge(T.sem[s], v)

@@ -2,13 +2,12 @@ from concourse.mybir import AluOpType, AxisListType, ActivationFunctionType
 
 W, B, RO = 3712, 160, 4
 UN = 464
-SCH = [(0, 56), (56, 112), (112, 144)]
-VCH = (144, 160)
+SCH = [(0, 56), (56, 112), (112, 144), (144, 160)]
 OFF = 4352.0
 M32 = 402653184.0
 M16 = 201326592.0
 M16K = 1.5 * 2.0 ** 37
-BIG = 2.0 ** 40
+AC = (17.0 - 15.5, 17.0)
 
 SCRATCH = {
     "ilt": ("sbuf", [128, W], "int32"), "tmp": ("sbuf", [128, W], "int32"),
@@ -16,28 +15,34 @@ SCRATCH = {
     "colt": ("sbuf", [128, W], "bfloat16"),
     "vv": ("sbuf", [128, 16 * B], "bfloat16"), "mn": ("sbuf", [128, 16 * B], "bfloat16"), "mx": ("sbuf", [128, 4 * B], "bfloat16"),
     "eq": ("sbuf", [128, 10 * B], "bfloat16"), "dru": ("sbuf", [128, B], "uint16"),
-    "y0t": ("sbuf", [128, B], "bfloat16"), "lt": ("sbuf", [128, 64], "int32"), "ltf": ("sbuf", [128, 64], "float32"), "ltt": ("sbuf", [128, 64], "float32"),
+    "y0t": ("sbuf", [128, B], "bfloat16"),
+    "ln8": ("sbuf", [8, B], "int32"), "tk8": ("sbuf", [8, B], "int32"), "ti8": ("sbuf", [8, B], "int32"), "th8": ("sbuf", [8, B], "int32"),
+    "lb8": ("sbuf", [8, B], "bfloat16"), "tb8": ("sbuf", [8, B], "bfloat16"), "tc8": ("sbuf", [8, B], "bfloat16"),
+    "sel": ("sbuf", [8, 128], "bfloat16"), "sel32": ("sbuf", [8, 128], "bfloat16"), "tf0": ("sbuf", [128, 10], "float32"),
+    "ac": ("sbuf", [128, 2], "float32"), "awm": ("sbuf", [128, 10], "float32"), "thr": ("sbuf", [128, 10], "float32"),
     "wg": ("sbuf", [128, B], "bfloat16"), "wgi": ("sbuf", [128, B], "int32"), "lg": ("sbuf", [128, B], "bfloat16"), "cg": ("sbuf", [128, B], "bfloat16"), "sg": ("sbuf", [128, B], "bfloat16"),
     "st": ("sbuf", [128, B], "uint16"), "kk": ("sbuf", [128, B], "bfloat16"),
     "ui": ("sbuf", [128, B], "int32"), "ui2": ("sbuf", [128, B], "int32"), "wold": ("sbuf", [128, B], "bfloat16"),
     "dws": ("sbuf", [128, B], "float32"), "ps": ("sbuf", [128, B], "float32"), "rs": ("sbuf", [128, B], "float32"), "qs": ("sbuf", [128, B], "float32"),
     "lose": ("sbuf", [128, 10], "float32"), "lose2": ("sbuf", [128, 10], "float32"), "dd": ("sbuf", [128, 10], "float32"),
     "d0": ("sbuf", [128, 120], "float32"), "d1": ("sbuf", [128, 120], "float32"), "po": ("sbuf", [128, 120], "float32"),
-    "ta1": ("sbuf", [128, 10], "float32"), "ta2": ("sbuf", [128, 10], "float32"), "ta3": ("sbuf", [128, 10], "float32"), "ta4": ("sbuf", [128, 10], "float32"),
+    "ta4": ("sbuf", [128, 10], "float32"),
     "acol": ("sbuf", [128, 1], "float32"), "ai": ("sbuf", [128, 1], "int32"), "ai2": ("sbuf", [128, 1], "int32"), "am": ("sbuf", [128, 1], "float32"),
     "tfa": ("sbuf", [128, 10], "float32"), "qi": ("sbuf", [128, 10], "int32"), "qi2": ("sbuf", [128, 10], "int32"), "tfn": ("sbuf", [128, 10], "float32"),
-    "aw0": ("sbuf", [128, 10], "uint16"), "tki": ("sbuf", [128, 10], "int32"), "tki2": ("sbuf", [128, 10], "int32"), "l32": ("sbuf", [128, 10], "float32"), "af": ("sbuf", [128, 10], "float32"),
+    "aw0": ("sbuf", [128, 10], "uint16"),
     "fi": ("sbuf", [128, 20], "int32"), "fi2": ("sbuf", [128, 20], "int32"), "ft": ("sbuf", [128, 32], "float32"), "ftt": ("sbuf", [128, 32], "float32"),
-    "ones": ("sbuf", [128, 128], "bfloat16"), "g1": ("sbuf", [128, 128], "bfloat16"), "gb": ("sbuf", [128, 128], "bfloat16"), "i1": ("sbuf", [128, 128], "bfloat16"),
+    "ones": ("sbuf", [128, 224], "bfloat16"), "g1": ("sbuf", [128, 128], "bfloat16"), "gb": ("sbuf", [128, 128], "bfloat16"), "i1": ("sbuf", [128, 128], "bfloat16"),
     "i32": ("sbuf", [128, 128], "bfloat16"), "in1": ("sbuf", [128, 128], "bfloat16"), "in16": ("sbuf", [128, 128], "bfloat16"),
-    "g8": ("sbuf", [128, 128], "bfloat16"), "gbig": ("sbuf", [128, 128], "bfloat16"), "gw": ("sbuf", [128, 128], "bfloat16"),
+    "g8": ("sbuf", [128, 128], "bfloat16"), "gw": ("sbuf", [128, 128], "bfloat16"),
     "e15": ("sbuf", [128, 128], "bfloat16"), "e15x": ("sbuf", [128, 128], "bfloat16"), "e15n": ("sbuf", [128, 128], "bfloat16"),
     "ea": ("sbuf", [128, 128], "bfloat16"), "eb": ("sbuf", [128, 128], "bfloat16"), "one5": ("sbuf", [128, 128], "float32"),
     "pq": ("sbuf", [128, B], "int32"), "pq2": ("sbuf", [128, B], "int32"), "mask": ("sbuf", [128, B], "bfloat16"), "q16": ("sbuf", [128, B], "float32"), "rsw": ("sbuf", [128, B], "float32"),
-    "r4": ("sbuf", [128, 896], "bfloat16"), "rs1": ("sbuf", [128, 896], "bfloat16"), "rs2": ("sbuf", [128, 224], "bfloat16"),
-    "pm0": ("sbuf", [128, 10], "int32"), "pm": ("sbuf", [128, 10], "int32"), "pmf": ("sbuf", [128, 10], "float32"), "c16": ("sbuf", [128, 10], "int32"),
+    "rs1": ("sbuf", [128, 896], "bfloat16"), "rs2": ("sbuf", [128, 224], "bfloat16"),
+    "pm0": ("sbuf", [128, 10], "int32"), "pm": ("sbuf", [128, 10], "int32"), "c16": ("sbuf", [128, 10], "int32"),
     "li": ("sbuf", [128, 10], "float32"), "li16": ("sbuf", [128, 10], "float32"), "dum": ("sbuf", [128, 10], "float32"),
-    "cc": ("sbuf", [128, 24], "float32"), "bt": ("sbuf", [128, 8], "int32"),
+    "gwa": ("sbuf", [128, 1280], "bfloat16"), "e0": ("sbuf", [128, 128], "bfloat16"), "e0x": ("sbuf", [128, 128], "bfloat16"),
+    "half": ("sbuf", [128, 32], "float32"), "rv": ("sbuf", [128, 16], "float32"), "rv2": ("sbuf", [128, 16], "float32"), "rv3": ("sbuf", [128, 16], "float32"),
+    "y2": ("sbuf", [128, B], "bfloat16"), "kk2": ("sbuf", [128, B], "bfloat16"),
 }
 for _t in range(RO):
     SCRATCH["m1_%d" % _t] = ("sbuf", [128, 20], "uint16")
@@ -48,7 +53,7 @@ for _t in range(RO):
     SCRATCH["r3_%d" % _t] = ("sbuf", [128, 20], "uint16")
 for _t in range(8):
     SCRATCH["b%d" % _t] = ("psum", [128, 512], "float32")
-SEMAPHORES = ["qV", "qS", "qT", "qP", "loc", "dil0", "dil1", "dil2", "dil3", "dx", "dy", "dlt", "oyy", "oyw", "osm", "osn"]
+SEMAPHORES = ["qV", "qS", "qT", "qP", "loc", "dil0", "dil1", "dil2", "dil3", "dx", "dy", "dln", "dtk", "oyy", "oyw", "osm", "osn"]
 SEMAPHORES += ["a%s_%d" % (m, t) for m in ("1", "z", "3") for t in range(RO)]
 
 
@@ -124,8 +129,12 @@ def rank_program(g, core, T, topo):
     def mm(out, lhs, rhs, start, stop, r, w):
         do("T", lambda v: v.matmul(out, lhs, rhs, start, stop), r, w)
 
-    def act(out, in_, func, r, w, bias=None):
-        if bias is None:
+    def act(out, in_, func, r, w, bias=None, scale=None):
+        if scale is not None and bias is not None:
+            do("S", lambda v: v.activation(out, in_, func, bias=bias, scale=scale), r, w)
+        elif scale is not None:
+            do("S", lambda v: v.activation(out, in_, func, scale=scale), r, w)
+        elif bias is None:
             do("S", lambda v: v.activation(out, in_, func), r, w)
         else:
             do("S", lambda v: v.activation(out, in_, func, bias=bias), r, w)
@@ -144,91 +153,105 @@ def rank_program(g, core, T, topo):
         lastw[tok] = [(sem, na, {sem: na})]
         tot[sem] = na
 
-    ms(T.lt[:], 0, ["lt"])
+    dma("Y", T.ln8[:], T.ln0[:], [], ["ln8"], "dln")
+    dma("Y", T.tk8[:], T.tk0[:], [], ["tk8"], "dtk")
     for q in range(4):
         c = q * 928
         dma("Y", T.ilt[:, c:c + 928], T.il[:, c:c + 928], [], ["il%d" % q], "dil%d" % q)
     dma("Y", T.xt[:], T.xw[:], [], ["x"], "dx")
-    lts = []
-    for a in range(4):
-        for h in range(2):
-            for j, src in ((0, T.ln0), (1, T.tk0)):
-                tk = "lt%d%d%d" % (a, h, j)
-                lastw[tk] = lastw["lt"]
-                dma("S", T.lt[32 * a:32 * a + 10, 32 * j + 16 * h:32 * j + 16 * h + 16], src[2 * a + h:2 * a + h + 1, :], [], [tk], "dlt")
-                lts.append(tk)
     dma("S", T.y0t[:], T.y0[:], [], ["y0"], "dy")
 
     def pool(fn, r, w):
         do("P", fn, r, w)
     ms(T.ones[:], 1.0, ["ones"])
     pool(lambda p: p.iota(T.pq[:], [[0, 10], [1, 16]], 128, -1), [], ["pq"])
+    pool(lambda p: p.iota(T.q16[:], [[0, 10], [1, 16]], 0, 0, allow_small_or_imprecise_dtypes=True), [], ["q16"])
+    pool(lambda p: p.affine_select(T.i1[:], T.ones[:, 0:128], [[-1, 128]], EQ, 0.0, 0, 1), ["ones"], ["i1"])
+    pool(lambda p: p.affine_select(T.sel[:], T.ones[0:8, 0:128], [[1, 8], [0, 16]], EQ, 0.0, 0, -1), ["ones"], ["sel"])
     pool(lambda p: p.iota(T.pm0[:], [[0, 10]], 0, 1), [], ["pm0"])
     pool(lambda p: p.iota(T.c16[:], [[16, 10]], 0, 0), [], ["c16"])
-    pool(lambda p: p.iota(T.q16[:], [[0, 10], [1, 16]], 0, 0, allow_small_or_imprecise_dtypes=True), [], ["q16"])
-    pool(lambda p: p.affine_select(T.i1[:], T.ones[:], [[-1, 128]], EQ, 0.0, 0, 1), ["ones"], ["i1"])
-    pool(lambda p: p.affine_select(T.gb[:], T.ones[:], [[-16, 8], [0, 16]], GE, 0.0, 0, 1), ["ones"], ["gb"])
+    pool(lambda p: p.iota(T.colt[:, 0:928], [[0, 29], [1, 32]], -16, 0, allow_small_or_imprecise_dtypes=True), [], ["colt0"])
+    pool(lambda p: p.affine_select(T.gb[:], T.ones[:, 0:128], [[-16, 8], [0, 16]], GE, 0.0, 0, 1), ["ones"], ["gb"])
     pool(lambda p: p.affine_select(T.g1[:], T.gb[:], [[16, 8], [0, 16]], GE, 0.0, 15, -1), ["gb"], ["g1"])
-    pool(lambda p: p.iota(T.r4[:], [[0, 224], [1, 4]], 0, 0, allow_small_or_imprecise_dtypes=True), [], ["r4"])
-    pool(lambda p: p.iota(T.colt[:], [[0, 116], [1, 32]], -16, 0, allow_small_or_imprecise_dtypes=True), [], ["colt"])
 
-    ms(T.wy[:, W:W + B], 0.0, ["wyd"])
-    ms(T.ft[:], 0.0, ["ft"])
-    ms(T.one5[:], 512.0, ["one5"])
-    ms(T.acol[:], 0.0, ["acol"])
-    ms(T.am[:], 0.0, ["am"])
-    ms(T.d0[:], 1.0, ["d0c"])
-    ms(T.d1[:], 0.0, ["d1c"])
-    d0c = lambda lo, hi, v: ms(T.d0[:, lo:hi:6], v, ["d0c"])
-    d0c(0, 60, 0.0); d0c(5, 60, -1.0)
-    d0c(60, 120, 0.0); d0c(61, 120, 0.0); d0c(62, 120, 0.0); d0c(65, 120, -1.0)
-    d1c = lambda lo, hi, v: ms(T.d1[:, lo:hi:6], v, ["d1c"])
-    d1c(3, 60, M32); d1c(4, 60, -M32); d1c(63, 120, M16); d1c(64, 120, -M16)
+    def fill(ap, n_, v, w):
+        act(ap, T.ones[:, 0:n_], AF.Copy, ["ones"], [w], scale=v)
+    fill(T.half[:, 0:16], 16, 0.5, "half")
+    fill(T.half[:, 16:32], 16, 0.0, "half")
+    fill(T.d0[:], 120, 1.0, "d0c")
+    for lo, hi, v in ((0, 60, 0.0), (5, 60, -1.0), (60, 120, 0.0), (61, 120, 0.0), (62, 120, 0.0), (65, 120, -1.0)):
+        fill(T.d0[:, lo:hi:6], 10, v, "d0c")
+    fill(T.d1[:], 120, 0.0, "d1c")
+    for lo, hi, v in ((3, 60, M32), (4, 60, -M32), (63, 120, M16), (64, 120, -M16)):
+        fill(T.d1[:, lo:hi:6], 10, v, "d1c")
     for k in ("d1b", "d1s", "d1x1", "d1x2", "d1x3", "d1x4"):
         lastw[k] = lastw["d1c"]
     lastw["d0s"] = lastw["d0c"]
+    fill(T.rs2[:], 224, 0.0, "rs2")
+    Q4 = [[0, 56], [1, 4]]
+    pool(lambda p: p.affine_select(T.rs1[:, 0:224], T.rs2[:], Q4, OP.not_equal, 512.0, 0, 0), ["rs2"], ["rs1_0"])
+    pool(lambda p: p.affine_select(T.rs2[:], T.rs2[:], Q4, EQ, 512.0, 0, 0), ["rs2"], ["rs2"])
+    CT = ["colt%d" % j for j in range(4)]
+
     ts(T.pq2[:], T.pq[:], 15, AND, ["pq"], ["pq2"])
     ts(T.mask[:], T.pq2[:], 0.0, GT, ["pq2"], ["mask"], -(2.0 ** 60), MUL)
     ts(T.rsw[:], T.q16[:], -0.5, ADD, ["q16"], ["rsw"], 1e27, MUL)
+    act(T.sel32[:], T.sel[:], AF.Copy, ["sel"], ["sel32"], scale=32.0)
+    cp(T.lb8[:], T.ln8[:], ["ln8"], ["lb8"])
+    ts(T.ti8[:], T.tk8[:], 31, AND, ["tk8"], ["ti8"])
+    ts(T.th8[:], T.tk8[:], 5, SHR, ["tk8"], ["th8"])
+    cp(T.tb8[:], T.ti8[:], ["ti8"], ["tb8"])
+    cp(T.tc8[:], T.th8[:], ["th8"], ["tc8"])
+    for bb, tb, hi, thi in ((T.b0, "b0", T.lb8, "lb8"), (T.b1, "b1", T.tc8, "tc8")):
+        mm(bb[:, 0:B], T.i1[:], T.mask[:], True, False, ["i1", "mask"], [tb])
+        mm(bb[:, 0:B], T.sel32[:], hi[:], False, False, ["sel32", thi], [tb])
+        mm(bb[:, 0:B], T.sel[:], T.tb8[:], False, True, ["sel", "tb8"], [tb])
+    scan(T.qs[:], T.rsw[:], T.b0[:, 0:B], MIN, MAX, ["rsw", "b0"], ["qs"])
+    cp(T.aw0[:], T.qs[:, 15:B:16], ["qs"], ["aw_0"])
+    scan(T.ps[:], T.rsw[:], T.b1[:, 0:B], MIN, MAX, ["rsw", "b1"], ["ps"])
+    cp(T.tf0[:], T.ps[:, 15:B:16], ["ps"], ["tf0"])
+
+    GP = [[-16, 8], [0, 16]]
+    pool(lambda p: p.affine_select(T.e15[:], T.ones[:, 0:128], GP, EQ, 0.0, -15, 1), ["ones"], ["e15"])
+    pool(lambda p: p.affine_select(T.e0[:], T.ones[:, 0:128], GP, EQ, 0.0, 0, 1), ["ones"], ["e0"])
+    act(T.i32[:], T.i1[:], AF.Copy, ["i1"], ["i32"], scale=32.0)
+    act(T.in16[:], T.i1[:], AF.Copy, ["i1"], ["in16"], scale=-16.0)
+    for j in range(1, 4):
+        act(T.colt[:, 928 * j:928 * j + 928], T.colt[:, 0:928], AF.Copy, ["colt0"], ["colt%d" % j])
+    act(T.cg[:], T.colt[:].indirect(T.aw0[:]), AF.Copy, CT + ["aw_0"], ["cg"])
+    act(T.e15x[:], T.e15[:], AF.Copy, ["e15"], ["e15x"], scale=32.0)
+    act(T.e15n[:], T.e15[:], AF.Copy, ["e15"], ["e15n"], scale=-16.0)
+    act(T.e0x[:], T.e0[:], AF.Copy, ["e0"], ["e0x"], scale=16384.0)
+    pool(lambda p: p.affine_select(T.ea[:], T.e0x[:], GP, OP.not_equal, -16384.0, -1, 1), ["e0x"], ["ea"])
+    act(T.eb[:], T.e0[:], AF.Copy, ["e0"], ["eb"], scale=32.0)
+    act(T.in1[:], T.i1[:], AF.Copy, ["i1"], ["in1"], scale=-1.0)
+    act(T.g8[:], T.g1[:], AF.Copy, ["g1"], ["g8"], scale=8192.0)
     ts(T.pm[:], T.pm0[:], 15, AND, ["pm0"], ["pm"])
-    cp(T.pmf[:], T.pm[:], ["pm"], ["pmf"])
     tt(T.li[:], T.pm[:], T.c16[:], ADD, ["pm", "c16"], ["li"])
-    ts(T.li16[:], T.li[:], 16.0, MUL, ["li"], ["li16"], OFF, ADD)
-    ts(T.dum[:], T.li[:], W + OFF, ADD, ["li"], ["dum"])
-    ts(T.i32[:], T.i1[:], 32.0, MUL, ["i1"], ["i32"])
-    ts(T.in1[:], T.i1[:], -1.0, MUL, ["i1"], ["in1"])
-    ts(T.in16[:], T.i1[:], -16.0, MUL, ["i1"], ["in16"])
-    ts(T.g8[:], T.g1[:], 8192.0, MUL, ["g1"], ["g8"])
-    ts(T.gbig[:], T.g1[:], BIG, MUL, ["g1"], ["gbig"])
-    cc = lambda j: T.cc[:, j:j + 1]
-    pf = T.pmf[:, 0:1]
-    ts(cc(0), pf, 15.0, EQ, ["pmf"], ["cc0"])
-    ts(cc(1), pf, 0.0, EQ, ["pmf"], ["cc1"])
-    ts(cc(2), pf, 1.0, EQ, ["pmf"], ["cc2"])
-    tt(cc(3), cc(1), cc(2), SUB, ["cc1", "cc2"], ["cc3"])
-    ts(T.e15[:], T.g1[:], cc(0), MUL, ["g1", "cc0"], ["e15"])
-    ts(T.e15x[:], T.g1[:], cc(0), MUL, ["g1", "cc0"], ["e15x"], 32.0, MUL)
-    ts(T.e15n[:], T.g1[:], cc(0), MUL, ["g1", "cc0"], ["e15n"], -16.0, MUL)
-    ts(T.ea[:], T.g1[:], cc(3), MUL, ["g1", "cc3"], ["ea"], 16384.0, MUL)
-    ts(T.eb[:], T.g1[:], cc(1), MUL, ["g1", "cc1"], ["eb"], 32.0, MUL)
-    for k in range(4):
-        f = float(4 ** (2 ** k))
-        ts(T.bt[:, k:k + 1], T.pm[:, 0:1], k, SHR, ["pm"], ["bt%d" % k], 1, AND)
-        ts(cc(4 + k), T.bt[:, k:k + 1], 1.0 - f, MUL, ["bt%d" % k], ["cc%d" % (4 + k)], f, ADD)
-    tt(cc(8), cc(4), cc(5), MUL, ["cc4", "cc5"], ["cc8"])
-    tt(cc(9), cc(6), cc(7), MUL, ["cc6", "cc7"], ["cc9"])
-    tt(cc(10), cc(8), cc(9), MUL, ["cc8", "cc9"], ["cc10"])
-    ts(cc(11), cc(10), 2.0, MUL, ["cc10"], ["cc11"])
-    ts(T.gw[:], T.g1[:], cc(10), MUL, ["g1", "cc10"], ["gw"])
-    ts(T.rs1[:], T.r4[:], 0.0, EQ, ["r4"], ["rs1"], 512.0, MUL)
-    ts(T.rs2[:], T.r4[:, 0:224], 0.0, GT, ["r4"], ["rs2"], 512.0, MUL)
-    cp(T.ltf[:], T.lt[:], ["lt"] + lts, ["ltf"])
-    do("V", lambda v: v.transpose(T.ltt[:], T.ltf[:]), ["ltf"], ["ltt"])
-    cp(T.tki[:], T.ltt[:, 32:42], ["ltt"], ["tki"])
-    ts(T.l32[:], T.ltt[:, 0:10], 32.0, MUL, ["ltt"], ["l32"])
-    ts(T.tki2[:], T.tki[:], 31, AND, ["tki"], ["tki2"])
-    tt(T.af[:], T.l32[:], T.tki2[:], ADD, ["l32", "tki2"], ["af"])
-    cp(T.aw0[:], T.af[:], ["af"], ["aw_0"])
+    do("V", lambda v: v.tensor_tensor_scan(T.rv[:], T.half[:, 0:16], T.half[:, 16:32], 65536.0, MUL, ADD), ["half"], ["rv"])
+    tt(T.rv2[:], T.rv[:], T.mask[:, 0:16], ADD, ["rv", "mask"], ["rv2"])
+    scan(T.rv3[:], T.rsw[:, 0:16], T.rv2[:], MIN, MAX, ["rsw", "rv2"], ["rv3"])
+    wc = T.rv3[:, 15:16]
+    act(T.gw[:], T.g1[:], AF.Copy, ["g1", "rv3"], ["gw"], scale=wc)
+    for c in range(10):
+        act(T.gwa[:, 128 * c:128 * c + 128], T.gw[:], AF.Copy, ["gw"], ["gw%d" % c], scale=2.0 ** (24 - 16 * c))
+
+    def late_fills():
+        for c in range(10):
+            act(T.thr[:, c:c + 1], wc, AF.Copy, ["rv3"], ["thr"], scale=2.5 * 2.0 ** (24 - 16 * c))
+        act(T.li16[:], T.li[:], AF.Identity, ["li"], ["li16"], bias=OFF + 17.0, scale=16.0)
+        act(T.dum[:], T.li[:], AF.Identity, ["li"], ["dum"], bias=W + OFF, scale=1.0)
+        fill(T.acol[:], 1, 0.0, "acol")
+        fill(T.am[:], 1, 0.0, "am")
+        for j, v in enumerate(AC):
+            fill(T.ac[:, j:j + 1], 1, v, "ac%d" % j)
+        act(T.ta4[:], T.li16[:], AF.Identity, ["li16"], ["ta4"], bias=0.0, scale=1.0)
+        fill(T.ft[:], 32, 0.0, "ft")
+        fill(T.one5[:], 128, 512.0, "one5")
+        fill(T.wy[:, W:W + B], B, 0.0, "wyd")
+    for j in range(1, 4):
+        act(T.rs1[:, 224 * j:224 * j + 224], T.rs1[:, 0:224], AF.Copy, ["rs1_0"], ["rs1_%d" % j])
+    RS1 = ["rs1_%d" % j for j in range(4)]
 
     WY = ["wy%d" % u for u in range(8)] + ["wyd"]
     IL = ["il0", "il1", "il2", "il3"]
@@ -246,6 +269,11 @@ def rank_program(g, core, T, topo):
         cp(T.wold[:], T.wy[:].indirect(d), WY + ["r1_%d" % (t - 1)], ["wold"])
         mm(T.b2[:, 0:B], T.i1[:], T.wold[:], True, True, ["i1", "wold"], ["b2"])
 
+    def skips_mod():
+        cp(T.ai[:], T.acol[:], ["acol"], ["ai"])
+        ts(T.ai2[:], T.ai[:], 31, AND, ["ai"], ["ai2"])
+        cp(T.am[:], T.ai2[:], ["ai2"], ["am"])
+
     def rewrite(t):
         tz = "rz_%d" % (t - 1)
         d = T["r1_%d" % (t - 1)][:, 0:10]
@@ -260,92 +288,109 @@ def rank_program(g, core, T, topo):
         m1, zs, m3 = T["m1_%d" % t], T["zs_%d" % t], T["m3_%d" % t]
         if t == 0:
             y, ty, aw, taw = T.y0t[:], "y0", T.aw0[:], "aw_0"
-            tfin, ttf = T.ltt[:, 32:42], "ltt"
+            tfin, ttf = T.tf0[:], "tf0"
         else:
             y, ty = T["rz_%d" % (t - 1)][:], "rz_%d" % (t - 1)
             aw, taw = T["r3_%d" % (t - 1)][:, 0:10], "r3_%d" % (t - 1)
             tfin, ttf = T["r1_%d" % t][:, 10:20], "r1_%d" % t
         for k, s in (("r1", "a1"), ("rz", "az"), ("r3", "a3")):
             arrives("%s_%d" % (k, t), "%s_%d" % (s, t))
-        mm(b[6][:, 0:B], T.i1[:], y, True, True, ["i1", ty], ["b6"])
         for j in (3, 4, 5, 7):
             mm(P(j), T.i1[:], T.mask[:], True, False, ["i1", "mask"], ["b%d" % j])
         if t > 0:
             rewrite(t)
+        if t > 0:
+            act(T.cg[:], T.colt[:].indirect(aw), AF.Copy, CT + [taw], ["cg"])
         if t == 0:
             ts(T.wgi[:], T.ilt[:].indirect(aw), 31, AND, IL + [taw], ["wgi"])
-            cp(T.wg[:], T.wgi[:], ["wgi"], ["wg"])
+            ts(T.lg[:], T.ilt[:].indirect(aw), 0.03125, MUL, IL + [taw], ["lg"], 136.0 - 31.0 / 64.0, ADD)
+            tt(T.wg[:], T.wgi[:], T.cg[:], ADD, ["wgi", "cg"], ["wg"])
         else:
-            cp(T.wg[:], T.wy[:].indirect(aw), WY + [taw], ["wg"])
-        act(T.cg[:], T.colt[:].indirect(aw), AF.Copy, ["colt", taw], ["cg"])
-        ts(T.lg[:], T.ilt[:].indirect(aw), 0.03125, MUL, IL + [taw], ["lg"], 136.0 - 31.0 / 64.0, ADD)
-        if t > 0:
+            ts(T.lg[:], T.ilt[:].indirect(aw), 0.03125, MUL, IL + [taw], ["lg"], 136.0 - 31.0 / 64.0, ADD)
+            tt(T.wg[:], T.wy[:].indirect(aw), T.cg[:], ADD, WY + [taw, "cg"], ["wg"])
             cp(T.xt[:, 0:16 * B].indirect(T["r3_%d" % (t - 1)][:, 10:20]), y, [ty, taw], ["x"])
-        mm(P(0), T.i1[:], T.wg[:], True, False, ["i1", "wg"], ["b0"])
-        mm(P(0), T.i1[:], T.cg[:], False, True, ["i1", "cg"], ["b0"])
-        act(T.sg[:], P(0), AF.Sign, ["b0"], ["sg"], bias=-15.5)
-        mm(P(1), T.i1[:], T.wg[:], True, False, ["i1", "wg"], ["b1"])
-        mm(P(1), T.i1[:], T.cg[:], False, False, ["i1", "cg"], ["b1"])
-        mm(P(1), T.i32[:], T.lg[:], False, False, ["i32", "lg"], ["b1"])
-        mm(P(1), T.in16[:], T.sg[:], False, True, ["in16", "sg"], ["b1"])
-        for j, first in ((2, True), (3, False)):
-            mm(P(j), T.e15[:], T.wg[:], first, False, ["e15", "wg"], ["b%d" % j])
-            mm(P(j), T.e15[:], T.cg[:], False, False, ["e15", "cg"], ["b%d" % j])
-            mm(P(j), T.e15x[:], T.lg[:], False, False, ["e15x", "lg"], ["b%d" % j])
-            mm(P(j), T.e15n[:], T.sg[:], False, True, ["e15n", "sg"], ["b%d" % j])
-        mm(P(4), T.ea[:], T.lg[:], False, False, ["ea", "lg"], ["b4"])
-        mm(P(4), T.eb[:], T.lg[:], False, True, ["eb", "lg"], ["b4"])
+        ts(T.y2[:], y, 2.0, MUL, [ty], ["y2"], 0.5, MAX)
+        ts(T.awm[:], aw, -16.0 - 4096.0, ADD, [taw], ["awm"])
+        act(T.sg[:], T.wg[:], AF.Sign, ["wg"], ["sg"], bias=-15.5)
+
+        def part(j, what, first, stop):
+            lhs = {"l": ("i32", "e15x"), "w": ("i1", "e15"), "s": ("in16", "e15n")}[what][j > 1]
+            k = what + "g"
+            mm(P(j), T[lhs][:], T[k][:], first, stop, [lhs, k], ["b%d" % j])
+        part(1, "l", True, False)
+        part(2, "l", True, False)
+        part(1, "w", False, False)
+        part(2, "w", False, False)
+        part(1, "s", False, True)
+        part(2, "s", False, True)
+        part(3, "l", False, False)
+        part(3, "w", False, False)
+        part(3, "s", False, True)
         ts(T.st[:], P(1), -OFF, ADD, ["b1"], ["st"])
         for j, (lo, hi) in enumerate(SCH):
             act(T.vv[:, 16 * lo:16 * hi], T.xt[:].indirect(T.st[:, lo:hi]), AF.Copy, ["x", "st"], ["vv%d" % j])
         if t == 0:
+            late_fills()
             unit(5)
             unit(6)
         cp(T.dru[:], P(2), ["b2"], ["dru"])
+        if t > 0:
+            skips_mod()
         scan(T.dws[:], T.rsw[:], P(3), MIN, MAX, ["rsw", "b3"], ["dws"])
         for c in range(10):
             nn = B - 16 * c
             e0 = c * B
             ts(T.eq[:, e0:e0 + nn], T.dru[:, 16 * c:B], T.dws[:, 16 * c + 15:16 * c + 16], EQ, ["dru", "dws"], ["eq%d" % c])
-            mm(b[5][:, 16 * c:16 * c + 16], T.gw[:], T.eq[:, e0:e0 + 16], False, c == 9, ["gw", "eq%d" % c], ["b5"])
-            if c < 9:
-                mm(b[5][:, 16 * c + 16:B], T.gbig[:], T.eq[:, e0 + 16:e0 + nn], False, False, ["gbig", "eq%d" % c], ["b5"])
-        lo, hi = VCH
-        cp(T.vv[:, 16 * lo:16 * hi], T.xt[:].indirect(T.st[:, lo:hi]), ["x", "st"], ["vv3"])
-        scan(T.ps[:], T.rsw[:], P(4), MIN, MAX, ["rsw", "b4"], ["ps"])
-        ts(T.d0[:, 1:60:6], T.ps[:, 15:B:16], M16K, ADD, ["ps"], ["d0s"], M16K, SUB)
+            mm(b[5][:, 16 * c:B], T.gwa[:, 128 * c:128 * c + 128], T.eq[:, e0:e0 + nn], False, c == 9, ["gw%d" % c, "eq%d" % c], ["b5"])
+        mm(b[0][:, 256:256 + B], T.i1[:], T.y2[:], True, True, ["i1", "y2"], ["b0"])
+        mm(b[6][:, 256:256 + B], T.in1[:], y, True, False, ["in1", ty], ["b6"])
+        mm(P(4), T.ea[:], T.lg[:], False, False, ["ea", "lg"], ["b4"])
+        mm(P(4), T.eb[:], T.lg[:], False, True, ["eb", "lg"], ["b4"])
+        mm(P(7), T.i1[:], T.cg[:], False, False, ["i1", "cg"], ["b7"])
+
+        def min4(j):
+            lo, hi = SCH[j]
+            scan(T.mn[:, 16 * lo:16 * hi], T.rs1[:, 0:16 * (hi - lo)], T.vv[:, 16 * lo:16 * hi], MAX, MIN, RS1 + ["vv%d" % j], ["mn%d" % j])
+
+        def max4(j):
+            lo, hi = SCH[j]
+            scan(T.mx[:, 4 * lo:4 * hi], T.rs2[:, 0:4 * (hi - lo)], T.mn[:, 16 * lo + 3:16 * hi:4], MIN, MAX, ["rs2", "mn%d" % j], ["mx%d" % j])
+        min4(0)
         scan(T.rs[:], T.rsw[:], P(5), MIN, MAX, ["rsw", "b5"], ["rs"])
-        tt(T.d1[:, 1:60:6], T.d0[:, 1:60:6], T.ps[:, 15:B:16], SUB, ["d0s", "ps"], ["d1s"])
-        ts(T.lose[:], T.rs[:, 15:B:16], cc(11), GE, ["rs", "cc11"], ["lose"])
-        ts(T.ta1[:], aw, T.acol[:], ADD, [taw, "acol"], ["ta1"], 1.0 - 15.5, ADD)
-        ts(T.ta2[:], aw, T.acol[:], ADD, [taw, "acol"], ["ta2"], 1.0, ADD)
+        max4(0)
+        tt(T.lose[:], T.rs[:, 15:B:16], T.thr[:], GE, ["rs", "thr"], ["lose"])
+        min4(1)
         tt(T.lose2[:], T.lose[:], T.dum[:], MUL, ["lose", "dum"], ["lose2"])
-        if not last:
-            ts(T.ta3[:], aw, T.acol[:], ADD, [taw, "acol"], ["ta3"], 1.0 - 7.5, ADD)
-            tt(T.ta4[:], T.ta2[:], T.li16[:], ADD, ["ta2", "li16"], ["ta4"])
+        max4(1)
         tt(T.dd[:], T.lose2[:], T.dws[:, 15:B:16], MAX, ["lose2", "dws"], ["dd"])
+        min4(2)
         ts(m1[:, 0:10], T.dd[:], -OFF, ADD, ["dd"], ["m1d_%d" % t])
         wid = 10 if t == 0 else 20
         send(T["r1_%d" % t][:, 0:wid], m1[:, 0:wid], ["m1d_%d" % t] + (["m1t_%d" % t] if t else []), "a1_%d" % t)
-        for j, (lo, hi) in list(enumerate(SCH))[:-1] + [(3, VCH)] + [(2, SCH[2])]:
-            l = hi - lo
-            scan(T.mn[:, 16 * lo:16 * hi], T.rs1[:, 0:16 * l], T.vv[:, 16 * lo:16 * hi], MAX, MIN, ["rs1", "vv%d" % j], ["mn%d" % j])
-            scan(T.mx[:, 4 * lo:4 * hi], T.rs2[:, 0:4 * l], T.mn[:, 16 * lo + 3:16 * hi:4], MIN, MAX, ["rs2", "mn%d" % j], ["mx%d" % j])
-        mm(b[6][:, 256:256 + B], T.in1[:], y, True, False, ["in1", ty], ["b6"])
+        max4(2)
+        min4(3)
+        max4(3)
+        mall = T.mx[:, 3:4 * B:4]
+        mtok = ["mx0", "mx1", "mx2", "mx3"]
         mm(b[6][:, 256:256 + B], T.i1[:], T.mx[:, 3:4 * B:4], False, True, ["i1", "mx0", "mx1", "mx2", "mx3"], ["b6"])
         act(zs[:], b[6][:, 256:256 + B], AF.Abs, ["b6"], ["zs_%d" % t])
         send(T["rz_%d" % t][:], zs[:], ["zs_%d" % t], "az_%d" % t)
-        tt(T.kk[:], zs[:], b[6][:, 0:B], GE, ["zs_%d" % t, "b6"], ["kk"])
-        mm(P(7), T.g1[:], zs[:], False, False, ["g1", "zs_%d" % t], ["b7"])
-        mm(P(7), T.g8[:], T.kk[:], False, True, ["g8", "kk"], ["b7"])
+        ts(T.kk2[:], mall, 0.0, EQ, mtok, ["kk2"])
+        tt(T.kk[:], mall, b[0][:, 256:256 + B], GE, mtok + ["b0"], ["kk"])
+        scan(T.ps[:], T.rsw[:], P(4), MIN, MAX, ["rsw", "b4"], ["ps"])
+        ts(T.d0[:, 1:60:6], T.ps[:, 15:B:16], M16K, ADD, ["ps"], ["d0s"], M16K, SUB)
+        tt(T.d1[:, 1:60:6], T.d0[:, 1:60:6], T.ps[:, 15:B:16], SUB, ["d0s", "ps"], ["d1s"])
+        mm(P(7), T.g8[:], T.kk2[:], False, False, ["g8", "kk2"], ["b7"])
+        mm(P(7), T.g8[:], T.kk[:], False, False, ["g8", "kk"], ["b7"])
+        mm(P(7), T.g1[:], zs[:], False, True, ["g1", "zs_%d" % t], ["b7"])
         scan(T.qs[:], T.rsw[:], P(7), MIN, MAX, ["rsw", "b7"], ["qs"])
         q = T.qs[:, 15:B:16]
-        ts(T.d1[:, 0:60:6], q, 73727.5, GE, ["qs"], ["d1b"], 1.0 / 512.0, MUL)
-        tt(T.d1[:, 2:60:6], q, T.ta1[:], ADD, ["qs", "ta1"], ["d1x1"])
-        tt(T.d1[:, 5:60:6], q, T.ta2[:], ADD, ["qs", "ta2"], ["d1x2"])
+        act(T.d1[:, 2:60:6], q, AF.Identity, ["qs", "ac0"], ["d1x1"], bias=T.ac[:, 0:1])
+        act(T.d1[:, 5:60:6], q, AF.Identity, ["qs", "ac1"], ["d1x2"], bias=T.ac[:, 1:2])
+        ts(T.d1[:, 0:60:6], q, 73711.5, GE, ["qs"], ["d1b"], 1.0 / 512.0, MUL)
 
         def clock(out):
-            cp(T.qi[:], q, ["qs"], ["qi"])
+            tt(T.qi[:], q, T.awm[:], SUB, ["qs", "awm"], ["qi"])
             ts(T.tfa[:], tfin, T.am[:], ADD, [ttf, "am"], ["tfa"], 1.0, ADD)
             ts(T.qi2[:], T.qi[:], 31, AND, ["qi"], ["qi2"])
             tt(T.tfn[:], T.tfa[:], T.qi2[:], ADD, ["tfa", "qi2"], ["tfn"])
@@ -357,21 +402,20 @@ def rank_program(g, core, T, topo):
             clock((m3[:, 10:20], "m3b"))
             send(T["r3_%d" % t][:], m3[:], ["m3a", "m3b"], "a3_%d" % t)
         else:
-            tt(T.d1[:, 62:120:6], q, T.ta3[:], ADD, ["qs", "ta3"], ["d1x3"])
+            ts(T.d1[:, 62:120:6], q, T.acol[:], ADD, ["qs", "acol"], ["d1x3"], 17.0 - 7.5, ADD)
             tt(T.d1[:, 65:120:6], q, T.ta4[:], ADD, ["qs", "ta4"], ["d1x4"])
             scan(T.po[:], T.d0[:], T.d1[:], MUL, ADD, toks + ["d1x3", "d1x4"], ["po"])
             ts(m3[:], T.po[:, 5:120:6], -OFF, ADD, ["po"], ["m3_%d" % t])
             send(T["r3_%d" % t][:], m3[:], ["m3_%d" % t], "a3_%d" % t)
             mm(b[0][:, 0:10], T.one5[:], T.d1[:, 0:60:6], True, True, ["one5", "d1b"], ["b0"])
-            clock((T["m1_%d" % (t + 1)][:, 10:20], "m1t_%d" % (t + 1)))
-            do("V", lambda v: v.tensor_reduce(T.acol[:], b[0][:, 0:10], AxisListType.X, ADD), ["b0"], ["acol"])
             if t == 0:
                 unit(7)
+            clock((T["m1_%d" % (t + 1)][:, 10:20], "m1t_%d" % (t + 1)))
+            do("V", lambda v: v.tensor_reduce(T.acol[:], b[0][:, 0:10], AxisListType.X, ADD), ["b0"], ["acol"])
+            for j, v in enumerate(AC):
+                act(T.ac[:, j:j + 1], T.acol[:], AF.Identity, ["acol"], ["ac%d" % j], bias=v, scale=1.0)
+            act(T.ta4[:], T.li16[:], AF.Identity, ["li16", "acol"], ["ta4"], bias=T.acol[:], scale=1.0)
         rewrite_prep(t + 1)
-        if not last:
-            cp(T.ai[:], T.acol[:], ["acol"], ["ai"])
-            ts(T.ai2[:], T.ai[:], 31, AND, ["ai"], ["ai2"])
-            cp(T.am[:], T.ai2[:], ["ai2"], ["am"])
     rewrite(RO)
     dma("Y", T.yw[:], T.wy[:, 0:W], WY, [], "oyw")
     dma("S", T.yy[:], T["rz_3"][:], ["rz_3"], [], "oyy")

@@ -4,10 +4,11 @@ W, B, RO = 3712, 160, 4
 UN = 464
 SCH = [(0, 56), (56, 112), (112, 144), (144, 160)]
 OFF = 4352.0
+OFD = OFF - 16.0
 M32 = 402653184.0
 M16 = 201326592.0
 M16K = 1.5 * 2.0 ** 37
-AC = (17.0 - 15.5, 17.0)
+AC = (17.0 - 15.5, 17.0, 17.0 - 7.5)
 
 SCRATCH = {
     "ilt": ("sbuf", [128, W], "int32"), "tmp": ("sbuf", [128, W], "int32"),
@@ -19,7 +20,7 @@ SCRATCH = {
     "ln8": ("sbuf", [8, B], "int32"), "tk8": ("sbuf", [8, B], "int32"), "ti8": ("sbuf", [8, B], "int32"), "th8": ("sbuf", [8, B], "int32"),
     "lb8": ("sbuf", [8, B], "bfloat16"), "tb8": ("sbuf", [8, B], "bfloat16"), "tc8": ("sbuf", [8, B], "bfloat16"),
     "sel": ("sbuf", [8, 128], "bfloat16"), "sel32": ("sbuf", [8, 128], "bfloat16"), "tf0": ("sbuf", [128, 10], "float32"),
-    "ac": ("sbuf", [128, 2], "float32"), "awm": ("sbuf", [128, 10], "float32"), "thr": ("sbuf", [128, 10], "float32"),
+    "ac": ("sbuf", [128, 3], "float32"), "awm0": ("sbuf", [128, 10], "float32"), "awm1": ("sbuf", [128, 10], "float32"), "thr": ("sbuf", [128, 10], "float32"),
     "wg": ("sbuf", [128, B], "bfloat16"), "wgi": ("sbuf", [128, B], "int32"), "lg": ("sbuf", [128, B], "bfloat16"), "cg": ("sbuf", [128, B], "bfloat16"), "sg": ("sbuf", [128, B], "bfloat16"),
     "st": ("sbuf", [128, B], "uint16"), "kk": ("sbuf", [128, B], "bfloat16"),
     "ui": ("sbuf", [128, B], "int32"), "ui2": ("sbuf", [128, B], "int32"), "wold": ("sbuf", [128, B], "bfloat16"),
@@ -27,12 +28,12 @@ SCRATCH = {
     "lose": ("sbuf", [128, 10], "float32"), "lose2": ("sbuf", [128, 10], "float32"), "dd": ("sbuf", [128, 10], "float32"),
     "d0": ("sbuf", [128, 120], "float32"), "d1": ("sbuf", [128, 120], "float32"), "po": ("sbuf", [128, 120], "float32"),
     "ta4": ("sbuf", [128, 10], "float32"),
-    "acol": ("sbuf", [128, 1], "float32"), "ai": ("sbuf", [128, 1], "int32"), "ai2": ("sbuf", [128, 1], "int32"), "am": ("sbuf", [128, 1], "float32"),
+    "acol": ("sbuf", [128, 1], "float32"), "am1": ("sbuf", [128, 1], "float32"), "am2": ("sbuf", [128, 1], "float32"), "am3": ("sbuf", [128, 1], "float32"), "am": ("sbuf", [128, 2], "float32"),
     "tfa": ("sbuf", [128, 10], "float32"), "qi": ("sbuf", [128, 10], "int32"), "qi2": ("sbuf", [128, 10], "int32"), "tfn": ("sbuf", [128, 10], "float32"),
     "aw0": ("sbuf", [128, 10], "uint16"),
     "fi": ("sbuf", [128, 20], "int32"), "fi2": ("sbuf", [128, 20], "int32"), "ft": ("sbuf", [128, 32], "float32"), "ftt": ("sbuf", [128, 32], "float32"),
     "ones": ("sbuf", [128, 224], "bfloat16"), "g1": ("sbuf", [128, 128], "bfloat16"), "gb": ("sbuf", [128, 128], "bfloat16"), "i1": ("sbuf", [128, 128], "bfloat16"),
-    "i32": ("sbuf", [128, 128], "bfloat16"), "in1": ("sbuf", [128, 128], "bfloat16"), "in16": ("sbuf", [128, 128], "bfloat16"),
+    "i32": ("sbuf", [128, 128], "bfloat16"), "in1": ("sbuf", [128, 128], "bfloat16"),
     "g8": ("sbuf", [128, 128], "bfloat16"), "gw": ("sbuf", [128, 128], "bfloat16"),
     "e15": ("sbuf", [128, 128], "bfloat16"), "e15x": ("sbuf", [128, 128], "bfloat16"), "e15n": ("sbuf", [128, 128], "bfloat16"),
     "ea": ("sbuf", [128, 128], "bfloat16"), "eb": ("sbuf", [128, 128], "bfloat16"), "one5": ("sbuf", [128, 128], "float32"),
@@ -53,7 +54,7 @@ for _t in range(RO):
     SCRATCH["r3_%d" % _t] = ("sbuf", [128, 20], "uint16")
 for _t in range(8):
     SCRATCH["b%d" % _t] = ("psum", [128, 512], "float32")
-SEMAPHORES = ["qV", "qS", "qT", "qP", "loc", "dil0", "dil1", "dil2", "dil3", "dx", "dy", "dln", "dtk", "oyy", "oyw", "osm", "osn"]
+SEMAPHORES = ["qV", "qS", "qT", "qP", "loc", "dil0", "dil1", "dx", "dy", "dln", "dtk", "oyy", "oyw", "osm", "osn"]
 SEMAPHORES += ["a%s_%d" % (m, t) for m in ("1", "z", "3") for t in range(RO)]
 
 
@@ -155,9 +156,9 @@ def rank_program(g, core, T, topo):
 
     dma("Y", T.ln8[:], T.ln0[:], [], ["ln8"], "dln")
     dma("Y", T.tk8[:], T.tk0[:], [], ["tk8"], "dtk")
-    for q in range(4):
-        c = q * 928
-        dma("Y", T.ilt[:, c:c + 928], T.il[:, c:c + 928], [], ["il%d" % q], "dil%d" % q)
+    for q in range(2):
+        c = q * 1856
+        dma("Y", T.ilt[:, c:c + 1856], T.il[:, c:c + 1856], [], ["il%d" % q], "dil%d" % q)
     dma("Y", T.xt[:], T.xw[:], [], ["x"], "dx")
     dma("S", T.y0t[:], T.y0[:], [], ["y0"], "dy")
 
@@ -215,17 +216,17 @@ def rank_program(g, core, T, topo):
     pool(lambda p: p.affine_select(T.e15[:], T.ones[:, 0:128], GP, EQ, 0.0, -15, 1), ["ones"], ["e15"])
     pool(lambda p: p.affine_select(T.e0[:], T.ones[:, 0:128], GP, EQ, 0.0, 0, 1), ["ones"], ["e0"])
     act(T.i32[:], T.i1[:], AF.Copy, ["i1"], ["i32"], scale=32.0)
-    act(T.in16[:], T.i1[:], AF.Copy, ["i1"], ["in16"], scale=-16.0)
+    act(T.in1[:], T.i1[:], AF.Copy, ["i1"], ["in1"], scale=-1.0)
     for j in range(1, 4):
         act(T.colt[:, 928 * j:928 * j + 928], T.colt[:, 0:928], AF.Copy, ["colt0"], ["colt%d" % j])
     act(T.cg[:], T.colt[:].indirect(T.aw0[:]), AF.Copy, CT + ["aw_0"], ["cg"])
     act(T.e15x[:], T.e15[:], AF.Copy, ["e15"], ["e15x"], scale=32.0)
-    act(T.e15n[:], T.e15[:], AF.Copy, ["e15"], ["e15n"], scale=-16.0)
+    act(T.e15n[:], T.e15[:], AF.Copy, ["e15"], ["e15n"], scale=-1.0)
     act(T.e0x[:], T.e0[:], AF.Copy, ["e0"], ["e0x"], scale=16384.0)
     pool(lambda p: p.affine_select(T.ea[:], T.e0x[:], GP, OP.not_equal, -16384.0, -1, 1), ["e0x"], ["ea"])
     act(T.eb[:], T.e0[:], AF.Copy, ["e0"], ["eb"], scale=32.0)
-    act(T.in1[:], T.i1[:], AF.Copy, ["i1"], ["in1"], scale=-1.0)
     act(T.g8[:], T.g1[:], AF.Copy, ["g1"], ["g8"], scale=8192.0)
+    act(T.gb[:], T.g1[:], AF.Copy, ["g1", "gb"], ["g8n"], scale=-8192.0)
     ts(T.pm[:], T.pm0[:], 15, AND, ["pm0"], ["pm"])
     tt(T.li[:], T.pm[:], T.c16[:], ADD, ["pm", "c16"], ["li"])
     do("V", lambda v: v.tensor_tensor_scan(T.rv[:], T.half[:, 0:16], T.half[:, 16:32], 65536.0, MUL, ADD), ["half"], ["rv"])
@@ -240,9 +241,9 @@ def rank_program(g, core, T, topo):
         for c in range(10):
             act(T.thr[:, c:c + 1], wc, AF.Copy, ["rv3"], ["thr"], scale=2.5 * 2.0 ** (24 - 16 * c))
         act(T.li16[:], T.li[:], AF.Identity, ["li"], ["li16"], bias=OFF + 17.0, scale=16.0)
-        act(T.dum[:], T.li[:], AF.Identity, ["li"], ["dum"], bias=W + OFF, scale=1.0)
+        act(T.dum[:], T.li[:], AF.Identity, ["li"], ["dum"], bias=W + OFD, scale=1.0)
         fill(T.acol[:], 1, 0.0, "acol")
-        fill(T.am[:], 1, 0.0, "am")
+        fill(T.am[:, 0:1], 1, 0.0, "am0")
         for j, v in enumerate(AC):
             fill(T.ac[:, j:j + 1], 1, v, "ac%d" % j)
         act(T.ta4[:], T.li16[:], AF.Identity, ["li16"], ["ta4"], bias=0.0, scale=1.0)
@@ -254,25 +255,20 @@ def rank_program(g, core, T, topo):
     RS1 = ["rs1_%d" % j for j in range(4)]
 
     WY = ["wy%d" % u for u in range(8)] + ["wyd"]
-    IL = ["il0", "il1", "il2", "il3"]
+    IL = ["il0", "il1"]
 
     def unit(u):
         c = u * UN
-        ts(T.tmp[:, c:c + UN], T.ilt[:, c:c + UN], 31, AND, ["il%d" % (u // 2)], ["tmp%d" % u])
+        ts(T.tmp[:, c:c + UN], T.ilt[:, c:c + UN], 31, AND, ["il%d" % (u // 4)], ["tmp%d" % u])
         cp(T.wy[:, c:c + UN], T.tmp[:, c:c + UN], ["tmp%d" % u], ["wy%d" % u])
 
-    for u in range(5):
+    for u in range(4):
         unit(u)
 
     def rewrite_prep(t):
         d = T["r1_%d" % (t - 1)][:, 0:10]
         cp(T.wold[:], T.wy[:].indirect(d), WY + ["r1_%d" % (t - 1)], ["wold"])
         mm(T.b2[:, 0:B], T.i1[:], T.wold[:], True, True, ["i1", "wold"], ["b2"])
-
-    def skips_mod():
-        cp(T.ai[:], T.acol[:], ["acol"], ["ai"])
-        ts(T.ai2[:], T.ai[:], 31, AND, ["ai"], ["ai2"])
-        cp(T.am[:], T.ai2[:], ["ai2"], ["am"])
 
     def rewrite(t):
         tz = "rz_%d" % (t - 1)
@@ -299,6 +295,7 @@ def rank_program(g, core, T, topo):
             mm(P(j), T.i1[:], T.mask[:], True, False, ["i1", "mask"], ["b%d" % j])
         if t > 0:
             rewrite(t)
+        ts(T.y2[:], y, 2.0, MUL, [ty], ["y2"], 0.5, MAX)
         if t > 0:
             act(T.cg[:], T.colt[:].indirect(aw), AF.Copy, CT + [taw], ["cg"])
         if t == 0:
@@ -308,13 +305,14 @@ def rank_program(g, core, T, topo):
         else:
             ts(T.lg[:], T.ilt[:].indirect(aw), 0.03125, MUL, IL + [taw], ["lg"], 136.0 - 31.0 / 64.0, ADD)
             tt(T.wg[:], T.wy[:].indirect(aw), T.cg[:], ADD, WY + [taw, "cg"], ["wg"])
+        ts(T.sg[:], T.wg[:], 15.5, GE, ["wg"], ["sg"], 32.0, MUL)
+        if t > 0:
             cp(T.xt[:, 0:16 * B].indirect(T["r3_%d" % (t - 1)][:, 10:20]), y, [ty, taw], ["x"])
-        ts(T.y2[:], y, 2.0, MUL, [ty], ["y2"], 0.5, MAX)
-        ts(T.awm[:], aw, -16.0 - 4096.0, ADD, [taw], ["awm"])
-        act(T.sg[:], T.wg[:], AF.Sign, ["wg"], ["sg"], bias=-15.5)
+        else:
+            late_fills()
 
         def part(j, what, first, stop):
-            lhs = {"l": ("i32", "e15x"), "w": ("i1", "e15"), "s": ("in16", "e15n")}[what][j > 1]
+            lhs = {"l": ("i32", "e15x"), "w": ("i1", "e15"), "s": ("in1", "e15n")}[what][j > 1]
             k = what + "g"
             mm(P(j), T[lhs][:], T[k][:], first, stop, [lhs, k], ["b%d" % j])
         part(1, "l", True, False)
@@ -326,16 +324,13 @@ def rank_program(g, core, T, topo):
         part(3, "l", False, False)
         part(3, "w", False, False)
         part(3, "s", False, True)
-        ts(T.st[:], P(1), -OFF, ADD, ["b1"], ["st"])
+        ts(T.st[:], P(1), -OFD, ADD, ["b1"], ["st"])
         for j, (lo, hi) in enumerate(SCH):
             act(T.vv[:, 16 * lo:16 * hi], T.xt[:].indirect(T.st[:, lo:hi]), AF.Copy, ["x", "st"], ["vv%d" % j])
-        if t == 0:
-            late_fills()
-            unit(5)
-            unit(6)
         cp(T.dru[:], P(2), ["b2"], ["dru"])
         if t > 0:
-            skips_mod()
+            late[1](m1[:, 10:20], "m1t_%d" % t)
+        ts(T["awm%d" % (t % 2)][:], aw, -16.0 - 4096.0 - 131072.0, ADD, [taw], ["awm%d" % (t % 2)])
         scan(T.dws[:], T.rsw[:], P(3), MIN, MAX, ["rsw", "b3"], ["dws"])
         for c in range(10):
             nn = B - 16 * c
@@ -355,54 +350,76 @@ def rank_program(g, core, T, topo):
         def max4(j):
             lo, hi = SCH[j]
             scan(T.mx[:, 4 * lo:4 * hi], T.rs2[:, 0:4 * (hi - lo)], T.mn[:, 16 * lo + 3:16 * hi:4], MIN, MAX, ["rs2", "mn%d" % j], ["mx%d" % j])
-        min4(0)
+        if t:
+            min4(0)
+        else:
+            unit(4)
         scan(T.rs[:], T.rsw[:], P(5), MIN, MAX, ["rsw", "b5"], ["rs"])
-        max4(0)
+        if t:
+            max4(0)
         tt(T.lose[:], T.rs[:, 15:B:16], T.thr[:], GE, ["rs", "thr"], ["lose"])
-        min4(1)
+        if t:
+            min4(1)
         tt(T.lose2[:], T.lose[:], T.dum[:], MUL, ["lose", "dum"], ["lose2"])
-        max4(1)
+        if t:
+            max4(1)
         tt(T.dd[:], T.lose2[:], T.dws[:, 15:B:16], MAX, ["lose2", "dws"], ["dd"])
-        min4(2)
-        ts(m1[:, 0:10], T.dd[:], -OFF, ADD, ["dd"], ["m1d_%d" % t])
+        if t:
+            min4(2)
+        ts(m1[:, 0:10], T.dd[:], -OFD, ADD, ["dd"], ["m1d_%d" % t])
         wid = 10 if t == 0 else 20
         send(T["r1_%d" % t][:, 0:wid], m1[:, 0:wid], ["m1d_%d" % t] + (["m1t_%d" % t] if t else []), "a1_%d" % t)
+        if t == 0:
+            unit(5)
+            unit(6)
+            min4(0)
+            min4(1)
+            max4(0)
+            max4(1)
+            min4(2)
         max4(2)
         min4(3)
         max4(3)
         mall = T.mx[:, 3:4 * B:4]
         mtok = ["mx0", "mx1", "mx2", "mx3"]
         mm(b[6][:, 256:256 + B], T.i1[:], T.mx[:, 3:4 * B:4], False, True, ["i1", "mx0", "mx1", "mx2", "mx3"], ["b6"])
+        act(T.kk2[:], mall, AF.Sign, mtok, ["kk2"])
         act(zs[:], b[6][:, 256:256 + B], AF.Abs, ["b6"], ["zs_%d" % t])
         send(T["rz_%d" % t][:], zs[:], ["zs_%d" % t], "az_%d" % t)
-        ts(T.kk2[:], mall, 0.0, EQ, mtok, ["kk2"])
         tt(T.kk[:], mall, b[0][:, 256:256 + B], GE, mtok + ["b0"], ["kk"])
         scan(T.ps[:], T.rsw[:], P(4), MIN, MAX, ["rsw", "b4"], ["ps"])
         ts(T.d0[:, 1:60:6], T.ps[:, 15:B:16], M16K, ADD, ["ps"], ["d0s"], M16K, SUB)
         tt(T.d1[:, 1:60:6], T.d0[:, 1:60:6], T.ps[:, 15:B:16], SUB, ["d0s", "ps"], ["d1s"])
-        mm(P(7), T.g8[:], T.kk2[:], False, False, ["g8", "kk2"], ["b7"])
+        mm(P(7), T.gb[:], T.kk2[:], False, False, ["g8n", "kk2"], ["b7"])
         mm(P(7), T.g8[:], T.kk[:], False, False, ["g8", "kk"], ["b7"])
         mm(P(7), T.g1[:], zs[:], False, True, ["g1", "zs_%d" % t], ["b7"])
         scan(T.qs[:], T.rsw[:], P(7), MIN, MAX, ["rsw", "b7"], ["qs"])
         q = T.qs[:, 15:B:16]
         act(T.d1[:, 2:60:6], q, AF.Identity, ["qs", "ac0"], ["d1x1"], bias=T.ac[:, 0:1])
         act(T.d1[:, 5:60:6], q, AF.Identity, ["qs", "ac1"], ["d1x2"], bias=T.ac[:, 1:2])
-        ts(T.d1[:, 0:60:6], q, 73711.5, GE, ["qs"], ["d1b"], 1.0 / 512.0, MUL)
+        if not last:
+            act(T.d1[:, 62:120:6], q, AF.Identity, ["qs", "ac2"], ["d1x3"], bias=T.ac[:, 2:3])
+        ts(T.d1[:, 0:60:6], q, 73711.5 - 131072.0, GE, ["qs"], ["d1b"], 1.0 / 512.0, MUL)
 
-        def clock(out):
-            tt(T.qi[:], q, T.awm[:], SUB, ["qs", "awm"], ["qi"])
-            ts(T.tfa[:], tfin, T.am[:], ADD, [ttf, "am"], ["tfa"], 1.0, ADD)
+        h = t % 2
+        am, awm, tam, tawm = T.am[:, h:h + 1], T["awm%d" % h][:], "am%d" % h, "awm%d" % h
+
+        def clock1(q=q, am=am, awm=awm, tam=tam, tawm=tawm, tfin=tfin, ttf=ttf):
+            tt(T.qi[:], q, awm, SUB, ["qs", tawm], ["qi"])
+            ts(T.tfa[:], tfin, am, ADD, [ttf, tam], ["tfa"], 1.0, ADD)
             ts(T.qi2[:], T.qi[:], 31, AND, ["qi"], ["qi2"])
+
+        def clock2(out, tok):
             tt(T.tfn[:], T.tfa[:], T.qi2[:], ADD, ["tfa", "qi2"], ["tfn"])
-            cp(out[0], T.tfn[:], ["tfn"], [out[1]])
+            cp(out, T.tfn[:], ["tfn"], [tok])
         toks = ["d0c", "d0s", "d1c", "d1s", "d1b", "d1x1", "d1x2"]
         if last:
             scan(T.po[:, 0:60], T.d0[:, 0:60], T.d1[:, 0:60], MUL, ADD, toks, ["po"])
             ts(m3[:, 0:10], T.po[:, 5:60:6], -OFF, ADD, ["po"], ["m3a"])
-            clock((m3[:, 10:20], "m3b"))
+            clock1()
+            clock2(m3[:, 10:20], "m3b")
             send(T["r3_%d" % t][:], m3[:], ["m3a", "m3b"], "a3_%d" % t)
         else:
-            ts(T.d1[:, 62:120:6], q, T.acol[:], ADD, ["qs", "acol"], ["d1x3"], 17.0 - 7.5, ADD)
             tt(T.d1[:, 65:120:6], q, T.ta4[:], ADD, ["qs", "ta4"], ["d1x4"])
             scan(T.po[:], T.d0[:], T.d1[:], MUL, ADD, toks + ["d1x3", "d1x4"], ["po"])
             ts(m3[:], T.po[:, 5:120:6], -OFF, ADD, ["po"], ["m3_%d" % t])
@@ -410,12 +427,18 @@ def rank_program(g, core, T, topo):
             mm(b[0][:, 0:10], T.one5[:], T.d1[:, 0:60:6], True, True, ["one5", "d1b"], ["b0"])
             if t == 0:
                 unit(7)
-            clock((T["m1_%d" % (t + 1)][:, 10:20], "m1t_%d" % (t + 1)))
             do("V", lambda v: v.tensor_reduce(T.acol[:], b[0][:, 0:10], AxisListType.X, ADD), ["b0"], ["acol"])
             for j, v in enumerate(AC):
                 act(T.ac[:, j:j + 1], T.acol[:], AF.Identity, ["acol"], ["ac%d" % j], bias=v, scale=1.0)
             act(T.ta4[:], T.li16[:], AF.Identity, ["li16", "acol"], ["ta4"], bias=T.acol[:], scale=1.0)
+            act(T.am1[:], T.acol[:], AF.Identity, ["acol"], ["am1"], bias=-15.5, scale=1.0)
+            act(T.am2[:], T.am1[:], AF.Identity, ["am1"], ["am2"], bias=M32, scale=1.0)
+            act(T.am3[:], T.am2[:], AF.Identity, ["am2"], ["am3"], bias=-M32, scale=1.0)
+            act(T.am[:, 1 - h:2 - h], T.am3[:], AF.Identity, ["am3", "acol"], ["am%d" % (1 - h)], bias=T.acol[:], scale=-1.0)
+        late = (clock1, clock2)
         rewrite_prep(t + 1)
+        if not last:
+            clock1()
     rewrite(RO)
     dma("Y", T.yw[:], T.wy[:, 0:W], WY, [], "oyw")
     dma("S", T.yy[:], T["rz_3"][:], ["rz_3"], [], "oyy")

from concourse.mybir import AluOpType, AxisListType, ActivationFunctionType

W, B, RO = 3712, 160, 4
UN = 464
SCH = [(0, 56), (56, 112), (112, 144), (144, 160)]
OFF = 4352.0
OFD = OFF - 16.0
M32 = 402653184.0
M16 = 201326592.0
M16K = 1.5 * 2.0 ** 37
AC = (17.0 - 15.5, 17.0, 17.0 - 7.5)

SCRATCH = {
    "ilt": ("sbuf", [128, W], "int32"), "tmp": ("sbuf", [128, W], "int32"),
    "xt": ("sbuf", [128, W], "bfloat16"), "wy": ("sbuf", [128, W + B], "bfloat16"),
    "colt": ("sbuf", [128, W], "bfloat16"),
    "vv": ("sbuf", [128, 16 * B], "bfloat16"), "mn": ("sbuf", [128, 16 * B], "bfloat16"), "mx": ("sbuf", [128, 4 * B], "bfloat16"),
    "eq": ("sbuf", [128, 10 * B], "bfloat16"), "dru": ("sbuf", [128, B], "uint16"),
    "y0t": ("sbuf", [128, B], "bfloat16"),
    "ln8": ("sbuf", [8, B], "int32"), "tk8": ("sbuf", [8, B], "int32"), "ti8": ("sbuf", [8, B], "int32"), "th8": ("sbuf", [8, B], "int32"),
    "lb8": ("sbuf", [8, B], "bfloat16"), "tb8": ("sbuf", [8, B], "bfloat16"), "tc8": ("sbuf", [8, B], "bfloat16"),
    "sel": ("sbuf", [8, 128], "bfloat16"), "sel32": ("sbuf", [8, 128], "bfloat16"), "tf0": ("sbuf", [128, 10], "float32"),
    "ac": ("sbuf", [128, 3], "float32"), "awm0": ("sbuf", [128, 10], "float32"), "awm1": ("sbuf", [128, 10], "float32"), "thr": ("sbuf", [128, 10], "float32"),
    "wg": ("sbuf", [128, B], "bfloat16"), "wgi": ("sbuf", [128, B], "int32"), "lg": ("sbuf", [128, B], "bfloat16"), "cg": ("sbuf", [128, B], "bfloat16"), "sg": ("sbuf", [128, B], "bfloat16"),
    "st": ("sbuf", [128, B], "uint16"), "kk": ("sbuf", [128, B], "bfloat16"),
    "ui": ("sbuf", [128, B], "int32"), "ui2": ("sbuf", [128, B], "int32"), "wold": ("sbuf", [128, B], "bfloat16"),
    "dws": ("sbuf", [128, B], "float32"), "ps": ("sbuf", [128, B], "float32"), "rs": ("sbuf", [128, B], "float32"), "qs": ("sbuf", [128, B], "float32"),
    "lose": ("sbuf", [128, 10], "float32"), "lose2": ("sbuf", [128, 10], "float32"), "dd": ("sbuf", [128, 10], "float32"),
    "d0": ("sbuf", [128, 120], "float32"), "d1": ("sbuf", [128, 120], "float32"), "po": ("sbuf", [128, 120], "float32"),
    "ta4": ("sbuf", [128, 10], "float32"),
    "acol": ("sbuf", [128, 1], "float32"), "am1": ("sbuf", [128, 1], "float32"), "am2": ("sbuf", [128, 1], "float32"), "am3": ("sbuf", [128, 1], "float32"), "am": ("sbuf", [128, 2], "float32"),
    "tfa": ("sbuf", [128, 10], "float32"), "qi": ("sbuf", [128, 10], "int32"), "qi2": ("sbuf", [128, 10], "int32"), "tfn": ("sbuf", [128, 10], "float32"),
    "aw0": ("sbuf", [128, 10], "uint16"),
    "fi": ("sbuf", [128, 20], "int32"), "fi2": ("sbuf", [128, 20], "int32"), "ft": ("sbuf", [128, 32], "float32"), "ftt": ("sbuf", [128, 32], "float32"),
    "ones": ("sbuf", [128, 224], "bfloat16"), "g1": ("sbuf", [128, 128], "bfloat16"), "gb": ("sbuf", [128, 128], "bfloat16"), "i1": ("sbuf", [128, 128], "bfloat16"),
    "i32": ("sbuf", [128, 128], "bfloat16"), "in1": ("sbuf", [128, 128], "bfloat16"),
    "g8": ("sbuf", [128, 128], "bfloat16"), "gw": ("sbuf", [128, 128], "bfloat16"),
    "e15": ("sbuf", [128, 128], "bfloat16"), "e15x": ("sbuf", [128, 128], "bfloat16"), "e15n": ("sbuf", [128, 128], "bfloat16"),
    "ea": ("sbuf", [128, 128], "bfloat16"), "eb": ("sbuf", [128, 128], "bfloat16"), "one5": ("sbuf", [128, 128], "float32"),
    "pq": ("sbuf", [128, B], "int32"), "pq2": ("sbuf", [128, B], "int32"), "mask": ("sbuf", [128, B], "bfloat16"), "q16": ("sbuf", [128, B], "float32"), "rsw": ("sbuf", [128, B], "float32"),
    "rs1": ("sbuf", [128, 896], "bfloat16"), "rs2": ("sbuf", [128, 224], "bfloat16"),
    "pm0": ("sbuf", [128, 10], "int32"), "pm": ("sbuf", [128, 10], "int32"), "c16": ("sbuf", [128, 10], "int32"),
    "li": ("sbuf", [128, 10], "float32"), "li16": ("sbuf", [128, 10], "float32"), "dum": ("sbuf", [128, 10], "float32"),
    "gwa": ("sbuf", [128, 1280], "bfloat16"), "e0": ("sbuf", [128, 128], "bfloat16"), "e0x": ("sbuf", [128, 128], "bfloat16"),
    "half": ("sbuf", [128, 32], "float32"), "rv": ("sbuf", [128, 16], "float32"), "rv2": ("sbuf", [128, 16], "float32"), "rv3": ("sbuf", [128, 16], "float32"),
    "y2": ("sbuf", [128, B], "bfloat16"), "kk2": ("sbuf", [128, B], "bfloat16"),
}
for _t in range(RO):
    SCRATCH["m1_%d" % _t] = ("sbuf", [128, 20], "uint16")
    SCRATCH["zs_%d" % _t] = ("sbuf", [128, B], "bfloat16")
    SCRATCH["m3_%d" % _t] = ("sbuf", [128, 20], "uint16")
    SCRATCH["r1_%d" % _t] = ("sbuf", [128, 20], "uint16")
    SCRATCH["rz_%d" % _t] = ("sbuf", [128, B], "bfloat16")
    SCRATCH["r3_%d" % _t] = ("sbuf", [128, 20], "uint16")
for _t in range(8):
    SCRATCH["b%d" % _t] = ("psum", [128, 512], "float32")
SEMAPHORES = ["qV", "qS", "qT", "qP", "loc", "dil0", "dil1", "dx", "dy", "dln", "dtk", "oyy", "oyw", "osm", "osn"]
SEMAPHORES += ["a%s_%d" % (m, t) for m in ("1", "z", "3") for t in range(RO)]


def rank_program(g, core, T, topo):
    rank = T.rank_of(core)
    if rank is None:
        return
    n = len(T.cores)
    nxt, prv = T.cores[(rank + 1) % n], T.cores[(rank - 1) % n]
    OP, AF = AluOpType, ActivationFunctionType
    ADD, SUB, MUL, MAX, MIN, EQ, GE, GT = OP.add, OP.subtract, OP.mult, OP.max, OP.min, OP.is_equal, OP.is_ge, OP.is_gt
    AND, SHR = OP.bitwise_and, OP.arith_shift_right
    eng = {"V": g.vector, "S": g.scalar, "T": g.tensor, "P": g, "Y": g.sync}
    know = {e: {} for e in eng}
    tot, lastw, readers = {}, {}, {}

    def waits(e, r, w):
        deps = []
        for k in r:
            deps += lastw.get(k, [])
        for k in w:
            deps += lastw.get(k, []) + readers.get(k, [])
        deps = [d for d in deps if know[e].get(d[0], 0) < d[1] and not (e == "T" and d[0] == "qT")]
        need = {}
        for d in deps:
            if d[0] not in need or need[d[0]][1] < d[1]:
                need[d[0]] = d
        keep = [d for d in need.values() if not any(o is not d and o[2].get(d[0], 0) >= d[1] for o in need.values())]
        for d in keep:
            eng[e].wait_ge(T.sem[d[0]], d[1])
        for d in need.values():
            for s, v in list(d[2].items()) + [(d[0], d[1])]:
                know[e][s] = max(know[e].get(s, 0), v)

    def done(e, inst, r, w, sem, inc):
        tot[sem] = tot.get(sem, 0) + inc
        inst.then_inc(T.sem[sem], inc)
        snap = dict(know[e])
        snap[sem] = tot[sem]
        ev = (sem, tot[sem], snap)
        for k in r:
            readers.setdefault(k, []).append(ev)
        for k in w:
            lastw[k] = [ev]
            readers[k] = []

    def do(e, fn, r, w):
        waits(e, r, w)
        done(e, fn(eng[e]), r, w, "q" + e, 1)

    def dma(e, out, in_, r, w, sem):
        waits(e, r, w)
        done(e, eng[e].dma_start(out, in_), r, w, sem, 16)

    def tt(out, a, b, op, r, w):
        do("V", lambda v: v.tensor_tensor(out, a, b, op), r, w)

    def ts(out, a, s1, o1, r, w, s2=None, o2=None):
        if o2 is None:
            do("V", lambda v: v.tensor_scalar(out, a, s1, None, o1), r, w)
        else:
            do("V", lambda v: v.tensor_scalar(out, a, s1, s2, o1, o2), r, w)

    def cp(out, a, r, w):
        do("V", lambda v: v.tensor_copy(out, a), r, w)

    def ms(ap, val, w):
        do("V", lambda v: v.memset(ap, val), [], w)

    def scan(out, x0, x1, o0, o1, r, w):
        do("V", lambda v: v.tensor_tensor_scan(out, x0, x1, 0.0, o0, o1), r, w)

    def mm(out, lhs, rhs, start, stop, r, w):
        do("T", lambda v: v.matmul(out, lhs, rhs, start, stop), r, w)

    def act(out, in_, func, r, w, bias=None, scale=None):
        if scale is not None and bias is not None:
            do("S", lambda v: v.activation(out, in_, func, bias=bias, scale=scale), r, w)
        elif scale is not None:
            do("S", lambda v: v.activation(out, in_, func, scale=scale), r, w)
        elif bias is None:
            do("S", lambda v: v.activation(out, in_, func), r, w)
        else:
            do("S", lambda v: v.activation(out, in_, func, bias=bias), r, w)

    sent = [0]
    rid, pid, _se = topo.addr(nxt)
    msk, ne = topo.mask(core, nxt), len(topo.engines(core, nxt))
    na = len(topo.engines(prv, core))

    def send(out, in_, r, sem):
        waits("P", r, [])
        g.remote_dma(out, in_, T.sem[sem], T.sem.loc, pid, rid, msk)
        sent[0] += ne

    def arrives(tok, sem):
        lastw[tok] = [(sem, na, {sem: na})]
        tot[sem] = na

    dma("Y", T.ln8[:], T.ln0[:], [], ["ln8"], "dln")
    dma("Y", T.tk8[:], T.tk0[:], [], ["tk8"], "dtk")
    for q in range(2):
        c = q * 1856
        dma("Y", T.ilt[:, c:c + 1856], T.il[:, c:c + 1856], [], ["il%d" % q], "dil%d" % q)
    dma("Y", T.xt[:], T.xw[:], [], ["x"], "dx")
    dma("S", T.y0t[:], T.y0[:], [], ["y0"], "dy")

    def pool(fn, r, w):
        do("P", fn, r, w)
    ms(T.ones[:], 1.0, ["ones"])
    pool(lambda p: p.iota(T.pq[:], [[0, 10], [1, 16]], 128, -1), [], ["pq"])
    pool(lambda p: p.iota(T.q16[:], [[0, 10], [1, 16]], 0, 0, allow_small_or_imprecise_dtypes=True), [], ["q16"])
    pool(lambda p: p.affine_select(T.i1[:], T.ones[:, 0:128], [[-1, 128]], EQ, 0.0, 0, 1), ["ones"], ["i1"])
    pool(lambda p: p.affine_select(T.sel[:], T.ones[0:8, 0:128], [[1, 8], [0, 16]], EQ, 0.0, 0, -1), ["ones"], ["sel"])
    pool(lambda p: p.iota(T.pm0[:], [[0, 10]], 0, 1), [], ["pm0"])
    pool(lambda p: p.iota(T.c16[:], [[16, 10]], 0, 0), [], ["c16"])
    pool(lambda p: p.iota(T.colt[:, 0:928], [[0, 29], [1, 32]], -16, 0, allow_small_or_imprecise_dtypes=True), [], ["colt0"])
    pool(lambda p: p.affine_select(T.gb[:], T.ones[:, 0:128], [[-16, 8], [0, 16]], GE, 0.0, 0, 1), ["ones"], ["gb"])
    pool(lambda p: p.affine_select(T.g1[:], T.gb[:], [[16, 8], [0, 16]], GE, 0.0, 15, -1), ["gb"], ["g1"])

    def fill(ap, n_, v, w):
        act(ap, T.ones[:, 0:n_], AF.Copy, ["ones"], [w], scale=v)
    fill(T.half[:, 0:16], 16, 0.5, "half")
    fill(T.half[:, 16:32], 16, 0.0, "half")
    fill(T.d0[:], 120, 1.0, "d0c")
    for lo, hi, v in ((0, 60, 0.0), (5, 60, -1.0), (60, 120, 0.0), (61, 120, 0.0), (62, 120, 0.0), (65, 120, -1.0)):
        fill(T.d0[:, lo:hi:6], 10, v, "d0c")
    fill(T.d1[:], 120, 0.0, "d1c")
    for lo, hi, v in ((3, 60, M32), (4, 60, -M32), (63, 120, M16), (64, 120, -M16)):
        fill(T.d1[:, lo:hi:6], 10, v, "d1c")
    for k in ("d1b", "d1s", "d1x1", "d1x2", "d1x3", "d1x4"):
        lastw[k] = lastw["d1c"]
    lastw["d0s"] = lastw["d0c"]
    fill(T.rs2[:], 224, 0.0, "rs2")
    Q4 = [[0, 56], [1, 4]]
    pool(lambda p: p.affine_select(T.rs1[:, 0:224], T.rs2[:], Q4, OP.not_equal, 512.0, 0, 0), ["rs2"], ["rs1_0"])
    pool(lambda p: p.affine_select(T.rs2[:], T.rs2[:], Q4, EQ, 512.0, 0, 0), ["rs2"], ["rs2"])
    CT = ["colt%d" % j for j in range(4)]

    ts(T.pq2[:], T.pq[:], 15, AND, ["pq"], ["pq2"])
    ts(T.mask[:], T.pq2[:], 0.0, GT, ["pq2"], ["mask"], -(2.0 ** 60), MUL)
    ts(T.rsw[:], T.q16[:], -0.5, ADD, ["q16"], ["rsw"], 1e27, MUL)
    act(T.sel32[:], T.sel[:], AF.Copy, ["sel"], ["sel32"], scale=32.0)
    cp(T.lb8[:], T.ln8[:], ["ln8"], ["lb8"])
    ts(T.ti8[:], T.tk8[:], 31, AND, ["tk8"], ["ti8"])
    ts(T.th8[:], T.tk8[:], 5, SHR, ["tk8"], ["th8"])
    cp(T.tb8[:], T.ti8[:], ["ti8"], ["tb8"])
    cp(T.tc8[:], T.th8[:], ["th8"], ["tc8"])
    for bb, tb, hi, thi in ((T.b0, "b0", T.lb8, "lb8"), (T.b1, "b1", T.tc8, "tc8")):
        mm(bb[:, 0:B], T.i1[:], T.mask[:], True, False, ["i1", "mask"], [tb])
        mm(bb[:, 0:B], T.sel32[:], hi[:], False, False, ["sel32", thi], [tb])
        mm(bb[:, 0:B], T.sel[:], T.tb8[:], False, True, ["sel", "tb8"], [tb])
    scan(T.qs[:], T.rsw[:], T.b0[:, 0:B], MIN, MAX, ["rsw", "b0"], ["qs"])
    cp(T.aw0[:], T.qs[:, 15:B:16], ["qs"], ["aw_0"])
    scan(T.ps[:], T.rsw[:], T.b1[:, 0:B], MIN, MAX, ["rsw", "b1"], ["ps"])
    cp(T.tf0[:], T.ps[:, 15:B:16], ["ps"], ["tf0"])

    GP = [[-16, 8], [0, 16]]
    pool(lambda p: p.affine_select(T.e15[:], T.ones[:, 0:128], GP, EQ, 0.0, -15, 1), ["ones"], ["e15"])
    pool(lambda p: p.affine_select(T.e0[:], T.ones[:, 0:128], GP, EQ, 0.0, 0, 1), ["ones"], ["e0"])
    act(T.i32[:], T.i1[:], AF.Copy, ["i1"], ["i32"], scale=32.0)
    act(T.in1[:], T.i1[:], AF.Copy, ["i1"], ["in1"], scale=-1.0)
    for j in range(1, 4):
        act(T.colt[:, 928 * j:928 * j + 928], T.colt[:, 0:928], AF.Copy, ["colt0"], ["colt%d" % j])
    act(T.cg[:], T.colt[:].indirect(T.aw0[:]), AF.Copy, CT + ["aw_0"], ["cg"])
    act(T.e15x[:], T.e15[:], AF.Copy, ["e15"], ["e15x"], scale=32.0)
    act(T.e15n[:], T.e15[:], AF.Copy, ["e15"], ["e15n"], scale=-1.0)
    act(T.e0x[:], T.e0[:], AF.Copy, ["e0"], ["e0x"], scale=16384.0)
    pool(lambda p: p.affine_select(T.ea[:], T.e0x[:], GP, OP.not_equal, -16384.0, -1, 1), ["e0x"], ["ea"])
    act(T.eb[:], T.e0[:], AF.Copy, ["e0"], ["eb"], scale=32.0)
    act(T.g8[:], T.g1[:], AF.Copy, ["g1"], ["g8"], scale=8192.0)
    act(T.gb[:], T.g1[:], AF.Copy, ["g1", "gb"], ["g8n"], scale=-8192.0)
    ts(T.pm[:], T.pm0[:], 15, AND, ["pm0"], ["pm"])
    tt(T.li[:], T.pm[:], T.c16[:], ADD, ["pm", "c16"], ["li"])
    do("V", lambda v: v.tensor_tensor_scan(T.rv[:], T.half[:, 0:16], T.half[:, 16:32], 65536.0, MUL, ADD), ["half"], ["rv"])
    tt(T.rv2[:], T.rv[:], T.mask[:, 0:16], ADD, ["rv", "mask"], ["rv2"])
    scan(T.rv3[:], T.rsw[:, 0:16], T.rv2[:], MIN, MAX, ["rsw", "rv2"], ["rv3"])
    wc = T.rv3[:, 15:16]
    act(T.gw[:], T.g1[:], AF.Copy, ["g1", "rv3"], ["gw"], scale=wc)
    for c in range(10):
        act(T.gwa[:, 128 * c:128 * c + 128], T.gw[:], AF.Copy, ["gw"], ["gw%d" % c], scale=2.0 ** (24 - 16 * c))

    def late_fills():
        for c in range(10):
            act(T.thr[:, c:c + 1], wc, AF.Copy, ["rv3"], ["thr"], scale=2.5 * 2.0 ** (24 - 16 * c))
        act(T.li16[:], T.li[:], AF.Identity, ["li"], ["li16"], bias=OFF + 17.0, scale=16.0)
        act(T.dum[:], T.li[:], AF.Identity, ["li"], ["dum"], bias=W + OFD, scale=1.0)
        fill(T.acol[:], 1, 0.0, "acol")
        fill(T.am[:, 0:1], 1, 0.0, "am0")
        for j, v in enumerate(AC):
            fill(T.ac[:, j:j + 1], 1, v, "ac%d" % j)
        act(T.ta4[:], T.li16[:], AF.Identity, ["li16"], ["ta4"], bias=0.0, scale=1.0)
        fill(T.ft[:], 32, 0.0, "ft")
        fill(T.one5[:], 128, 512.0, "one5")
        fill(T.wy[:, W:W + B], B, 0.0, "wyd")
    for j in range(1, 4):
        act(T.rs1[:, 224 * j:224 * j + 224], T.rs1[:, 0:224], AF.Copy, ["rs1_0"], ["rs1_%d" % j])
    RS1 = ["rs1_%d" % j for j in range(4)]

    WY = ["wy%d" % u for u in range(8)] + ["wyd"]
    IL = ["il0", "il1"]

    def unit(u):
        c = u * UN
        ts(T.tmp[:, c:c + UN], T.ilt[:, c:c + UN], 31, AND, ["il%d" % (u // 4)], ["tmp%d" % u])
        cp(T.wy[:, c:c + UN], T.tmp[:, c:c + UN], ["tmp%d" % u], ["wy%d" % u])

    for u in range(4):
        unit(u)

    def rewrite_prep(t):
        d = T["r1_%d" % (t - 1)][:, 0:10]
        cp(T.wold[:], T.wy[:].indirect(d), WY + ["r1_%d" % (t - 1)], ["wold"])
        mm(T.b2[:, 0:B], T.i1[:], T.wold[:], True, True, ["i1", "wold"], ["b2"])

    def rewrite(t):
        tz = "rz_%d" % (t - 1)
        d = T["r1_%d" % (t - 1)][:, 0:10]
        tt(T.ui[:], T.b2[:, 0:B], T[tz][:], ADD, ["b2", tz], ["ui"])
        ts(T.ui2[:], T.ui[:], 31, AND, ["ui"], ["ui2"])
        cp(T.wy[:].indirect(d), T.ui2[:], ["ui2", "r1_%d" % (t - 1)], WY)

    b = [T["b%d" % j] for j in range(8)]
    P = lambda j: b[j][:, 0:B]
    for t in range(RO):
        last = t == RO - 1
        m1, zs, m3 = T["m1_%d" % t], T["zs_%d" % t], T["m3_%d" % t]
        if t == 0:
            y, ty, aw, taw = T.y0t[:], "y0", T.aw0[:], "aw_0"
            tfin, ttf = T.tf0[:], "tf0"
        else:
            y, ty = T["rz_%d" % (t - 1)][:], "rz_%d" % (t - 1)
            aw, taw = T["r3_%d" % (t - 1)][:, 0:10], "r3_%d" % (t - 1)
            tfin, ttf = T["r1_%d" % t][:, 10:20], "r1_%d" % t
        for k, s in (("r1", "a1"), ("rz", "az"), ("r3", "a3")):
            arrives("%s_%d" % (k, t), "%s_%d" % (s, t))
        for j in (3, 4, 5, 7):
            mm(P(j), T.i1[:], T.mask[:], True, False, ["i1", "mask"], ["b%d" % j])
        if t > 0:
            rewrite(t)
        ts(T.y2[:], y, 2.0, MUL, [ty], ["y2"], 0.5, MAX)
        if t > 0:
            act(T.cg[:], T.colt[:].indirect(aw), AF.Copy, CT + [taw], ["cg"])
        if t == 0:
            ts(T.wgi[:], T.ilt[:].indirect(aw), 31, AND, IL + [taw], ["wgi"])
            ts(T.lg[:], T.ilt[:].indirect(aw), 0.03125, MUL, IL + [taw], ["lg"], 136.0 - 31.0 / 64.0, ADD)
            tt(T.wg[:], T.wgi[:], T.cg[:], ADD, ["wgi", "cg"], ["wg"])
        else:
            ts(T.lg[:], T.ilt[:].indirect(aw), 0.03125, MUL, IL + [taw], ["lg"], 136.0 - 31.0 / 64.0, ADD)
            tt(T.wg[:], T.wy[:].indirect(aw), T.cg[:], ADD, WY + [taw, "cg"], ["wg"])
        ts(T.sg[:], T.wg[:], 15.5, GE, ["wg"], ["sg"], 32.0, MUL)
        if t > 0:
            cp(T.xt[:, 0:16 * B].indirect(T["r3_%d" % (t - 1)][:, 10:20]), y, [ty, taw], ["x"])
        else:
            late_fills()

        def part(j, what, first, stop):
            lhs = {"l": ("i32", "e15x"), "w": ("i1", "e15"), "s": ("in1", "e15n")}[what][j > 1]
            k = what + "g"
            mm(P(j), T[lhs][:], T[k][:], first, stop, [lhs, k], ["b%d" % j])
        part(1, "l", True, False)
        part(2, "l", True, False)
        part(1, "w", False, False)
        part(2, "w", False, False)
        part(1, "s", False, True)
        part(2, "s", False, True)
        part(3, "l", False, False)
        part(3, "w", False, False)
        part(3, "s", False, True)
        ts(T.st[:], P(1), -OFD, ADD, ["b1"], ["st"])
        for j, (lo, hi) in enumerate(SCH):
            act(T.vv[:, 16 * lo:16 * hi], T.xt[:].indirect(T.st[:, lo:hi]), AF.Copy, ["x", "st"], ["vv%d" % j])
        cp(T.dru[:], P(2), ["b2"], ["dru"])
        if t > 0:
            late[1](m1[:, 10:20], "m1t_%d" % t)
        ts(T["awm%d" % (t % 2)][:], aw, -16.0 - 4096.0 - 131072.0, ADD, [taw], ["awm%d" % (t % 2)])
        scan(T.dws[:], T.rsw[:], P(3), MIN, MAX, ["rsw", "b3"], ["dws"])
        for c in range(10):
            nn = B - 16 * c
            e0 = c * B
            ts(T.eq[:, e0:e0 + nn], T.dru[:, 16 * c:B], T.dws[:, 16 * c + 15:16 * c + 16], EQ, ["dru", "dws"], ["eq%d" % c])
            mm(b[5][:, 16 * c:B], T.gwa[:, 128 * c:128 * c + 128], T.eq[:, e0:e0 + nn], False, c == 9, ["gw%d" % c, "eq%d" % c], ["b5"])
        mm(b[0][:, 256:256 + B], T.i1[:], T.y2[:], True, True, ["i1", "y2"], ["b0"])
        mm(b[6][:, 256:256 + B], T.in1[:], y, True, False, ["in1", ty], ["b6"])
        mm(P(4), T.ea[:], T.lg[:], False, False, ["ea", "lg"], ["b4"])
        mm(P(4), T.eb[:], T.lg[:], False, True, ["eb", "lg"], ["b4"])
        mm(P(7), T.i1[:], T.cg[:], False, False, ["i1", "cg"], ["b7"])

        def min4(j):
            lo, hi = SCH[j]
            scan(T.mn[:, 16 * lo:16 * hi], T.rs1[:, 0:16 * (hi - lo)], T.vv[:, 16 * lo:16 * hi], MAX, MIN, RS1 + ["vv%d" % j], ["mn%d" % j])

        def max4(j):
            lo, hi = SCH[j]
            scan(T.mx[:, 4 * lo:4 * hi], T.rs2[:, 0:4 * (hi - lo)], T.mn[:, 16 * lo + 3:16 * hi:4], MIN, MAX, ["rs2", "mn%d" % j], ["mx%d" % j])
        if t:
            min4(0)
        else:
            unit(4)
        scan(T.rs[:], T.rsw[:], P(5), MIN, MAX, ["rsw", "b5"], ["rs"])
        if t:
            max4(0)
        tt(T.lose[:], T.rs[:, 15:B:16], T.thr[:], GE, ["rs", "thr"], ["lose"])
        if t:
            min4(1)
        tt(T.lose2[:], T.lose[:], T.dum[:], MUL, ["lose", "dum"], ["lose2"])
        if t:
            max4(1)
        tt(T.dd[:], T.lose2[:], T.dws[:, 15:B:16], MAX, ["lose2", "dws"], ["dd"])
        if t:
            min4(2)
        ts(m1[:, 0:10], T.dd[:], -OFD, ADD, ["dd"], ["m1d_%d" % t])
        wid = 10 if t == 0 else 20
        send(T["r1_%d" % t][:, 0:wid], m1[:, 0:wid], ["m1d_%d" % t] + (["m1t_%d" % t] if t else []), "a1_%d" % t)
        if t == 0:
            unit(5)
            unit(6)
            min4(0)
            min4(1)
            max4(0)
            max4(1)
            min4(2)
        max4(2)
        min4(3)
        max4(3)
        mall = T.mx[:, 3:4 * B:4]
        mtok = ["mx0", "mx1", "mx2", "mx3"]
        mm(b[6][:, 256:256 + B], T.i1[:], T.mx[:, 3:4 * B:4], False, True, ["i1", "mx0", "mx1", "mx2", "mx3"], ["b6"])
        act(T.kk2[:], mall, AF.Sign, mtok, ["kk2"])
        act(zs[:], b[6][:, 256:256 + B], AF.Abs, ["b6"], ["zs_%d" % t])
        send(T["rz_%d" % t][:], zs[:], ["zs_%d" % t], "az_%d" % t)
        tt(T.kk[:], mall, b[0][:, 256:256 + B], GE, mtok + ["b0"], ["kk"])
        scan(T.ps[:], T.rsw[:], P(4), MIN, MAX, ["rsw", "b4"], ["ps"])
        ts(T.d0[:, 1:60:6], T.ps[:, 15:B:16], M16K, ADD, ["ps"], ["d0s"], M16K, SUB)
        tt(T.d1[:, 1:60:6], T.d0[:, 1:60:6], T.ps[:, 15:B:16], SUB, ["d0s", "ps"], ["d1s"])
        mm(P(7), T.gb[:], T.kk2[:], False, False, ["g8n", "kk2"], ["b7"])
        mm(P(7), T.g8[:], T.kk[:], False, False, ["g8", "kk"], ["b7"])
        mm(P(7), T.g1[:], zs[:], False, True, ["g1", "zs_%d" % t], ["b7"])
        scan(T.qs[:], T.rsw[:], P(7), MIN, MAX, ["rsw", "b7"], ["qs"])
        q = T.qs[:, 15:B:16]
        act(T.d1[:, 2:60:6], q, AF.Identity, ["qs", "ac0"], ["d1x1"], bias=T.ac[:, 0:1])
        act(T.d1[:, 5:60:6], q, AF.Identity, ["qs", "ac1"], ["d1x2"], bias=T.ac[:, 1:2])
        if not last:
            act(T.d1[:, 62:120:6], q, AF.Identity, ["qs", "ac2"], ["d1x3"], bias=T.ac[:, 2:3])
        ts(T.d1[:, 0:60:6], q, 73711.5 - 131072.0, GE, ["qs"], ["d1b"], 1.0 / 512.0, MUL)

        h = t % 2
        am, awm, tam, tawm = T.am[:, h:h + 1], T["awm%d" % h][:], "am%d" % h, "awm%d" % h

        def clock1(q=q, am=am, awm=awm, tam=tam, tawm=tawm, tfin=tfin, ttf=ttf):
            tt(T.qi[:], q, awm, SUB, ["qs", tawm], ["qi"])
            ts(T.tfa[:], tfin, am, ADD, [ttf, tam], ["tfa"], 1.0, ADD)
            ts(T.qi2[:], T.qi[:], 31, AND, ["qi"], ["qi2"])

        def clock2(out, tok):
            tt(T.tfn[:], T.tfa[:], T.qi2[:], ADD, ["tfa", "qi2"], ["tfn"])
            cp(out, T.tfn[:], ["tfn"], [tok])
        toks = ["d0c", "d0s", "d1c", "d1s", "d1b", "d1x1", "d1x2"]
        if last:
            scan(T.po[:, 0:60], T.d0[:, 0:60], T.d1[:, 0:60], MUL, ADD, toks, ["po"])
            ts(m3[:, 0:10], T.po[:, 5:60:6], -OFF, ADD, ["po"], ["m3a"])
            clock1()
            clock2(m3[:, 10:20], "m3b")
            send(T["r3_%d" % t][:], m3[:], ["m3a", "m3b"], "a3_%d" % t)
        else:
            tt(T.d1[:, 65:120:6], q, T.ta4[:], ADD, ["qs", "ta4"], ["d1x4"])
            scan(T.po[:], T.d0[:], T.d1[:], MUL, ADD, toks + ["d1x3", "d1x4"], ["po"])
            ts(m3[:], T.po[:, 5:120:6], -OFF, ADD, ["po"], ["m3_%d" % t])
            send(T["r3_%d" % t][:], m3[:], ["m3_%d" % t], "a3_%d" % t)
            mm(b[0][:, 0:10], T.one5[:], T.d1[:, 0:60:6], True, True, ["one5", "d1b"], ["b0"])
            if t == 0:
                unit(7)
            do("V", lambda v: v.tensor_reduce(T.acol[:], b[0][:, 0:10], AxisListType.X, ADD), ["b0"], ["acol"])
            for j, v in enumerate(AC):
                act(T.ac[:, j:j + 1], T.acol[:], AF.Identity, ["acol"], ["ac%d" % j], bias=v, scale=1.0)
            act(T.ta4[:], T.li16[:], AF.Identity, ["li16", "acol"], ["ta4"], bias=T.acol[:], scale=1.0)
            act(T.am1[:], T.acol[:], AF.Identity, ["acol"], ["am1"], bias=-15.5, scale=1.0)
            act(T.am2[:], T.am1[:], AF.Identity, ["am1"], ["am2"], bias=M32, scale=1.0)
            act(T.am3[:], T.am2[:], AF.Identity, ["am2"], ["am3"], bias=-M32, scale=1.0)
            act(T.am[:, 1 - h:2 - h], T.am3[:], AF.Identity, ["am3", "acol"], ["am%d" % (1 - h)], bias=T.acol[:], scale=-1.0)
        late = (clock1, clock2)
        rewrite_prep(t + 1)
        if not last:
            clock1()
    rewrite(RO)
    dma("Y", T.yw[:], T.wy[:, 0:W], WY, [], "oyw")
    dma("S", T.yy[:], T["rz_3"][:], ["rz_3"], [], "oyy")
    cp(T.fi[:], T["r3_3"][:], ["r3_3"], ["fi"])
    ts(T.fi2[:, 0:10], T.fi[:, 0:10], 5, SHR, ["fi"], ["fi2a"])
    ts(T.fi2[:, 10:20], T.fi[:, 10:20], 4095, AND, ["fi"], ["fi2b"])
    cp(T.ft[:, 0:20], T.fi2[:], ["fi2a", "fi2b"], ["ft"])
    do("V", lambda v: v.transpose(T.ftt[:], T.ft[:]), ["ft"], ["ftt"])
    for a in range(4):
        for h in range(2):
            r = 2 * a + h
            dma("S", T.yl[r:r + 1, :], T.ftt[32 * a:32 * a + 10, 16 * h:16 * h + 16], ["ftt"], [], "osm")
            dma("Y", T.yt[r:r + 1, :], T.ftt[32 * a + 10:32 * a + 20, 16 * h:16 * h + 16], ["ftt"], [], "osn")
    g.wait_ge(T.sem.loc, sent[0])
    for s, v in tot.items():
        if know["P"].get(s, 0) < v:
            g.wait_ge(T.sem[s], v)
